import numpy as np, ml_dtypes
CORES = [10,34,74,98]
N = 4
BF = ml_dtypes.bfloat16
W, M, H, L, CAP, RO = 2048, 4096, 2048, 256, 56, 4
def sums(w, x):
    return np.add.reduce(w[..., 0:1] * x, axis=2) & 4095, np.add.reduce(w[..., 1:2] * x, axis=2) & 4095
def probe(w, lm, tl, mo, m):
    u, v = sums(w, m); a = (u * v) >> 5
    c = (a[:, :, None] + w[..., 2:3] * u[:, :, None]) & (W - 1)
    x = np.take_along_axis(lm, c.reshape(N, 8, 1, 16 * L), 3).reshape(N, 8, 16, 16, L)
    ok = np.all(x <= m[:, :, :, None], axis=2); has = np.any(ok, axis=2)
    g = np.take_along_axis(c, np.argmax(ok, axis=2)[:, :, None], 2)
    tg = np.take_along_axis(tl, g, 3); q = m - np.take_along_axis(lm, g, 3)
    y = np.take_along_axis(mo, tg.reshape(N, 8, 1, 16 * L), 3).reshape(N, 8, 16, 16, L)
    p = np.minimum(q[:, :, :, None] + y, 255).reshape(N, 8, 16, 16 * L)
    e, f = sums(w, p); h = (((e * f) >> 5) + e) & (H - 1)
    return a, c[:, :, 0], has, tg, p, h
def seek(sn, has, p, h):
    new = np.any(np.take_along_axis(sn, h[:, :, None], 3) != p, axis=2).reshape(N, 8, 16, L) & has[:, :, None]
    return np.any(new, axis=2), np.argmax(new, axis=2)
def first(key):
    o = np.argsort(key, axis=2, kind="stable"); s = np.take_along_axis(key, o, 2)
    b = np.ones(key.shape, bool); b[..., 1:] = s[..., 1:] != s[..., :-1]
    win = np.zeros(key.shape, bool); np.put_along_axis(win, o, b, 2); return win
def turn(st, pr, fill):
    lm, tl, sn, m, ct, ci = st; a, c0, has, tg, p, h = pr
    child, i = seek(sn, has, p, h); j = i * L + np.arange(L)
    pc = np.take_along_axis(p, j[:, :, None], 3); hc = np.take_along_axis(h, j, 2)
    win = first(np.where(child, hc, np.where(has, 2 ** 15 + np.arange(L), 2 ** 14 + c0)))
    wt = np.where(np.arange(16)[:, None] == ci[:, :, None], (a & (M - 1))[:, :, None], ct)
    lm, tl, sn = lm.copy(), tl.copy(), sn.copy()
    for r in range(N):
        for g in range(8):
            b = win[r, g] & child[r, g]; sn[r, g][:, hc[r, g, b]] = pc[r, g][:, b]
            b = win[r, g] & ~has[r, g]; lm[r, g][:, c0[r, g, b]] = m[r, g][:, b]; tl[r, g][:, c0[r, g, b]] = wt[r, g][:, b]
    nm, nt, ni = fill.copy(), tl[..., :L].copy(), np.zeros((N, 8, L), np.int64)
    for d in range(N):
        f = child & ((hc & (N - 1)) == d); f = f & (np.add.accumulate(f.astype(np.int64), axis=2) <= CAP)
        for r in range(N):
            for g in range(8):
                b = np.flatnonzero(f[r, g]); z = r * CAP + np.arange(b.size)
                nm[d, g][:, z] = pc[r, g][:, b]; nt[d, g][:, z] = tg[r, g][:, b]; ni[d, g, z] = i[r, g, b]
    return lm, tl, sn, nm, nt, ni
def mono(rng, n, den, top):
    return ((rng.random((N, 8, 16, n), dtype=np.float32) < den) * rng.integers(1, top + 1, (N, 8, 16, n), dtype=np.int32)).astype(np.int32)
def uneven(rng, n, den):
    v = np.exp2(8 * rng.random((N, 8, 1, n), dtype=np.float32) * rng.random((N, 8, 16, n), dtype=np.float32))
    return ((rng.random((N, 8, 16, n), dtype=np.float32) < den) * np.minimum(v, 255).astype(np.int32)).astype(np.int32)
def base(rng):
    w = np.tile(rng.integers(0, 128, (1, 8, 16, 3), dtype=np.int32), (N, 1, 1, 1)); dens = np.array([0.15, 0.5, 0.8, 1.0, 1.0])
    lm = mono(rng, W, rng.choice(np.array([0.2, 0.3, 0.5]), (N, 8, 1, W)), 160); mo = mono(rng, M, rng.choice(np.array([0.2, 0.4]), (N, 8, 1, M)), 120)
    tl = rng.integers(0, M, (N, 8, 16, W), dtype=np.int32)
    sn = np.where(rng.random((N, 8, 1, H)) < 0.5, -1, mono(rng, H, 0.5, 255)).astype(np.int32)
    m = mono(rng, L, rng.choice(dens, (N, 8, 1, L)), 255); fr = mono(rng, RO * L, rng.choice(dens, (N, 8, 1, RO * L)), 255)
    old = np.take_along_axis(m, rng.integers(0, L, (N, 8, 1, RO * L)), 3)
    return w, lm, tl, mo, sn, m, np.where(rng.random((N, 8, 1, RO * L)) < 0.3, old, fr)
def plant(rng, w, lm, tl, mo, sn, m, fr, until=1, n=L - N * CAP - 8):
    pr = probe(w, lm, tl, mo, m); a, c0, has, tg, p, h = pr; used = np.zeros((N, 8, H), bool)
    cnt = rng.choice(np.array([0, 1, 2, 5, 15, 16]), (N, 8, L), p=[0.5, 0.2, 0.15, 0.05, 0.05, 0.05])
    for r in range(N):
        for g in range(8):
            for k in (1, 2, 5, 15, 16):
                x = np.flatnonzero(has[r, g] & (cnt[r, g] == k)); j = (np.arange(k)[:, None] * L + x).reshape(-1)
                sn[r, g][:, h[r, g, j]] = p[r, g][:, j]; used[r, g, h[r, g, j]] = True
    st = (lm, tl, sn, m, tl[..., :L], np.zeros((N, 8, L), np.int64))
    for t in range(until):
        was, row = st[1], st[5]; st = turn(st, pr, fr[..., t * L:(t + 1) * L])
        pr = probe(w, st[0], st[1], mo, st[3])
    own = pr[0] & (M - 1); came = np.any(st[3] != fr[..., (until - 1) * L:until * L], axis=2)
    stale = ~pr[2] & ~came & (row > 0)
    lone = ~pr[2] & came; anew = ~pr[2] & ~came & ~stale & np.any(st[1][..., :L] != was[..., :L], axis=2)
    used = used | np.any(st[2] != sn, axis=2)
    for r in range(N):
        for g in range(8):
            x = np.flatnonzero(lone[r, g]); v = np.flatnonzero(anew[r, g])[:4]
            s0 = np.flatnonzero(stale[r, g])[:4]
            if x.size + v.size + s0.size == 0: continue
            o = np.concatenate([s0, v, np.resize(x, n - v.size - s0.size)]) if x.size else np.concatenate([s0, v])
            fr[r, g][:, until * L + N * CAP:until * L + N * CAP + o.size] = st[3][r, g][:, o]
            half = rng.random(x.size) < 0.5
            col = np.concatenate([st[4][r, g][:, x][np.arange(16)[:, None] < st[5][r, g, x]],
                own[r, g, x[half]], own[r, g, v]])
            for part, cs in ((True, own[r, g, x[~half]]), (False, col)):
                y = mo[r, g][:, cs]
                e = np.add.reduce(w[r, g, :, 0:1] * y, axis=0) & 4095; f = np.add.reduce(w[r, g, :, 1:2] * y, axis=0) & 4095
                z = (((e * f) >> 5) + e) & (H - 1); b = ~used[r, g, z]
                if part: y = np.where((y == 0) & (rng.random(y.shape) < rng.choice(np.array([0.1, 0.5]), (1, y.shape[1]))), -1, y)
                sn[r, g][:, z[b]] = y[:, b]
def pack(w, lm, tl, mo, sn, m, fr):
    d = {"lm": lm, "tl": tl, "mo": mo, "sn": sn, "fm": m, "fr": fr, "wk": w}
    return {k: np.ascontiguousarray(x.reshape(N, 128, -1)).astype(np.int32) if k in ("tl", "wk") else np.ascontiguousarray(x.reshape(N, 128, -1)).astype(np.float32).astype(BF) for k, x in d.items()}
def setup_inputs(rng):
    s = base(rng); plant(rng, *s); return pack(*s)
def setup_inputs_again(rng):
    w, lm, tl, mo, sn, m, fr = base(rng); w[:, 2, :, 2] = 0; w[:, 3, :, 0] = 0; lm[:, 0] = 255; lm[:, 1] = 0; lm[N - 1, 3, :, 0] = 0; sn[:] = -1
    few = np.tile(rng.integers(0, M, (1, 8, 1, 5), dtype=np.int32), (N, 1, 1, 1))
    tl = np.take_along_axis(few, rng.integers(0, 5, (N, 8, 16, W)), 3); tl[:, :, 7] = rng.integers(0, M, (N, 8, W))
    fr = np.take_along_axis(m, rng.integers(0, 12, (N, 8, 1, RO * L)), 3); m = np.take_along_axis(m, rng.integers(0, 12, (N, 8, 1, L)), 3)
    return pack(w, lm, tl, mo, sn, m, fr)
def setup_inputs_corners(rng):
    w, lm, tl, mo, sn, m, fr = base(rng)
    lm[:, :, 0] = np.where(np.any(lm > 0, axis=2), lm[:, :, 0], 1); tl[:, 5] = rng.choice(np.array([0, M - 1]), (N, 16, W))
    fr[..., ::7] = 0; fr[..., 3::7] = 255
    pool, to = [], []
    for z in range(2):
        x = mono(rng, L, 0.9, 255); pr = probe(w, lm, tl, mo, x); child, i = seek(sn, pr[2], pr[4], pr[5])
        hc = np.take_along_axis(pr[5], i * L + np.arange(L), 2); pool.append(x); to.append(np.where(child, hc & (N - 1), -1))
    pool = np.concatenate(pool, axis=3); to = np.concatenate(to, axis=2)
    for r in range(N):
        for g in range(8):
            left = L; lanes = []
            for e in range(N):
                n = int(rng.choice(np.array([0, 1, CAP - 1, CAP, CAP + 1, 2 * CAP])))
                if r == 0 and e == 0: n = (CAP, CAP + 1, CAP - 1, 0, 1, CAP, CAP + 1, 2 * CAP)[g]
                if r == N - 1 and e == 0: n = CAP
                x = np.flatnonzero(to[r, g] == (r + 1 + e) % N)[:min(n, left)]; lanes.append(x); left -= x.size
            x = np.concatenate(lanes); m[r, g] = 0; m[r, g][:, rng.permutation(L)[:x.size]] = pool[r, g][:, x]
    return pack(w, lm, tl, mo, sn, m, fr)
def setup_inputs_ends(rng):
    def sub(n, den):
        return 255 * (rng.random((N, 8, 16, n)) < den).astype(np.int32)
    w = 127 * rng.integers(0, 2, (8, 16, 3)); w[6, :, 0:2] = 127; w[7, :, 0:2] = 0; w[:, 0, 2] = 0; w[:, 15, 2] = 127
    w[7, 0:4, 0] = 127; w[7, 4:8, 1] = 127; w[7, 13:16, 0] = (127, 127, 3); w[7, 10:13, 1] = (127, 127, 3)
    w = np.tile(w[None], (N, 1, 1, 1)).astype(np.int32); dens = np.array([0.0, 0.3, 0.6, 0.9, 1.0])
    lm = sub(W, 0.15); mo = sub(M, 0.3); tl = (M - 1) * rng.integers(0, 2, (N, 8, 16, W))
    t = rng.integers(0, 3, (N, 8, 1, H)); sn = np.where(t == 0, -1, np.where(t == 1, 255, 256 * rng.integers(0, 2, (N, 8, 16, H)) - 1))
    m = sub(L, rng.choice(dens, (N, 8, 1, L))); fr = sub(RO * L, rng.choice(dens, (N, 8, 1, RO * L)))
    for x in (m, fr):
        x[..., 0] = 255; x[..., -1] = 255
        z = rng.random(x.shape[-1]) < 0.3; z[0] = True; z[-1] = True
        x[:, 7, 0:8][:, :, z] = 0; x[:, 7, 10:16][:, :, z] = 255
    return pack(w, lm, tl, mo, sn, m, fr)
def setup_inputs_late(rng):
    w, lm, tl, mo, sn, m, fr = base(rng)
    lm = mono(rng, W, rng.choice(np.array([0.5, 0.6]), (N, 8, 1, W)), 160)
    pool = mono(rng, 8192, 0.5, 255); u, v = sums(w, pool)
    aim = np.where(np.arange(8) % 2 == 1, H - 1, 0)[:, None]
    k = np.argmax(((((u * v) >> 5) + u) & (H - 1)) == aim, axis=2)
    mo[..., M - 1:] = np.take_along_axis(pool, k[:, :, None, None], 3); sn[..., 0] = -1; sn[..., H - 1] = -1
    x = mono(rng, 4, 0.6, 255); u, v = sums(w, x); c0 = (((u * v) >> 5) + w[:, :, 0, 2:3] * u) & (W - 1)
    np.put_along_axis(lm, c0[:, :, None], x, 3); np.put_along_axis(tl[:, :, 0], c0, M - 1, 2)
    for t in (1, 2):
        fr[..., t * L + N * CAP + 24:t * L + N * CAP + 28] = x
    one = mono(rng, 1, 0.4, 255)
    for g in (3, 4):
        fr[:, g, :, :L] = one[:, g]
    s = (w, lm, tl, mo, sn, m, fr); plant(rng, *s, until=2, n=24); return pack(*s)
def setup_inputs_spread(rng):
    w = np.tile((np.exp2(7 * rng.random((1, 8, 16, 3))) - 1).astype(np.int32), (N, 1, 1, 1)); dens = np.array([0.3, 0.7, 1.0])
    lm = uneven(rng, W, rng.choice(np.array([0.2, 0.4]), (N, 8, 1, W))); mo = uneven(rng, M, 0.4)
    tl = np.minimum(M * rng.random((N, 8, 16, W)) ** 3, M - 1).astype(np.int32); sn = uneven(rng, H, 0.7) - 1
    m = uneven(rng, L, rng.choice(dens, (N, 8, 1, L))); fr = uneven(rng, RO * L, rng.choice(dens, (N, 8, 1, RO * L)))
    s = (w, lm, tl, mo, sn, m, fr); plant(rng, *s); return pack(*s)
def check_inputs(d):
    bad = []
    for k, lo, hi in (("lm", 0, 255), ("tl", 0, M - 1), ("mo", 0, 255), ("sn", -1, 255), ("fm", 0, 255), ("fr", 0, 255), ("wk", 0, 127)):
        x = np.asarray(d[k]).astype(np.float32)
        if not (np.all(x >= lo) and np.all(x <= hi)): bad.append("range of " + k)
        elif np.any(x != np.floor(x)): bad.append("whole numbers in " + k)
    if np.any(d["wk"] != d["wk"][:1]): bad.append("wk alike on all ranks")
    return bad
def reference(lm, tl, mo, sn, fm, fr, wk):
    lead, tail, mon, seen, front, fill, w = [x.astype(np.float32).astype(np.int32).reshape(N, 8, 16, -1) for x in (lm, tl, mo, sn, fm, fr, wk)]
    st = (lead, tail, seen, front, tail[..., :L], np.zeros((N, 8, L), np.int64))
    for t in range(RO):
        st = turn(st, probe(w, st[0], st[1], mon, st[3]), fill[..., t * L:(t + 1) * L])
    return {"yl": st[0].reshape(N, 128, W).astype(np.float32).astype(BF), "yf": st[3].reshape(N, 128, L).astype(np.float32).astype(BF)}

@@ -1,0 +1,703 @@
+from concourse.bass import DstId, RemoteDMATransfer
+from concourse.mybir import dt, AluOpType as A, AxisListType, ActivationFunctionType as F
+
+N, W, H, L, CAP, RO, SL = 4, 2048, 2048, 256, 56, 4, 224
+DUMP = 256
+SW = DUMP + N * 256
+_B, _F, _H, _I, _U = "bfloat16", "float32", "float16", "int32", "uint16"
+_SB = {
+    "xlm": (W + L, _B), "xtl": (W + L, _I), "xmo": (4096, _B), "xsn": (H + L, _B), "sn0": (H, _B), "fm0": (L, _B),
+    "fr0": (RO * L, _B), "wk0": (3, _I), "wkf": (3, _F), "frs": (N * SL, _B), "win0": (SW, _B), "win1": (SW, _B), "win2": (SW, _B), "win3": (SW, _B),
+    "wint0": (SW, _F), "wint1": (SW, _F),
+    "L0": (L, _B), "L1": (L, _B), "L2": (L, _B), "L3": (L, _B), "L4": (L, _B), "TR0": (L, _F), "TR1": (L, _F), "TR2": (L, _F), "yfo": (L, _B),
+    "mp": (L, _B), "mT": (L, _B), "qT": (L, _B), "au": (32, _I), "am": (32, _I), "up": (16, _I), "av": (48, _I), "ci": (L, _I),
+    "cj": (L, _I), "XV": (48, _H), "XA": (256, _H), "tl0": (W, _I), "ti": (1152, _I), "tj": (1152, _I), "tk": (1152, _I), "tbl": (2304, _B),
+    "CL": (L, _U), "X": (4096, _B), "E": (4096, _B), "Y": (4096, _B), "P": (4096, _B), "NE": (4096, _B), "SX": (4096, _B),
+    "SC": (256, _F), "gi": (16, _I), "gj": (16, _I), "GV": (16, _H), "XG": (256, _H), "GL": (16, _U), "TG": (L, _U), "xg": (L, _B),
+    "hi": (512, _I), "hp": (256, _I), "hq": (256, _I), "hs": (256, _I), "hh": (256, _I), "hf": (256, _H), "HL": (256, _U), "Kh": (256, _F),
+    "k2": (256, _F), "SC2": (256, _F), "ki": (16, _I), "kj": (16, _I), "IV": (16, _H), "XI": (256, _B), "CHL": (16, _U), "CH": (L, _B),
+    "has": (16, _F), "kh": (16, _I), "ch": (16, _I), "cd": (16, _I), "nc": (16, _I), "dd": (16, _I), "OH": (80, _B),
+    "w3": (80, _H), "rin": (N * SL, _B), "XS": (256, _H), "sf": (16, _F), "SLL": (16, _U),
+    "TGp": (L, _F), "mk": (L, _F), "YT": (L, _F), "CT": (L, _I), "CTm": (L, _I),
+    "nh": (16, _F), "nn": (16, _F), "c0i": (16, _I), "c0j": (16, _I), "lq": (16, _F), "sq": (16, _F),
+}
+for _z in "ls":
+    for _k, _v in {"y": (16, _F), "V2": (16, _H), "XW": (256, _H), "WA": (16, _U), "FT0": (L, _B), "FT1": (L, _B), "SCW": (1024, _B), "nd": (16, _F),
+                   "z": (16, _F), "V3": (16, _H), "XV": (256, _H), "WL": (16, _U)}.items():
+        _SB[_k + _z] = _v
+_CO = {
+    "one": (2048, _B), "I": (128, _B), "nI": (128, _B), "Ih": (128, _H), "bo": (128, _B), "b8": (8, _B), "tmp": (128, _B), "tri": (128, _B),
+    "Rep": (512, _B), "RepN": (512, _B), "Sel": (2048, _B), "Selh": (2048, _H), "R8": (128, _B), "TR": (128, _B), "key": (128, _B),
+    "key18": (128, _B), "r16": (128, _F), "cC": (8, _B), "lane": (16, _F), "base": (80, _B),
+    "mkc": (512, _B), "pc": (8, _F), "pi": (4, _I), "Wb": (128, _B), "Wt": (16, _B), "cT": (256, _F), "NB8": (8, _B), "PB8": (8, _B),
+    "c32": (32, _F), "duT": (16, _F), "dlT": (16, _F), "e0": (128, _F), "e1": (128, _F), "e2": (128, _F), "ek": (128, _F), "ea": (128, _F),
+    "EC": (128, _H), "EA": (128, _H),
+}
+_PACK, _POS = {}, {}
+for _k in list(_SB) + list(_CO):
+    _n, _t = (_SB.get(_k) or _CO.get(_k))
+    if _n <= 64:
+        _nn = max(32, (_n + 31) // 32 * 32)
+        _o = _PACK.get(_t, 0)
+        _POS[_k] = ("pk_" + _t, _o)
+        _PACK[_t] = _o + _nn
+    else:
+        _POS[_k] = ("t_" + _k, 0)
+SCRATCH = {}
+for _k in list(_SB) + list(_CO):
+    _n, _t = (_SB.get(_k) or _CO.get(_k))
+    if _n > 64:
+        SCRATCH["t_" + _k] = ("sbuf", [128, _n], _t)
+for _t, _n in _PACK.items():
+    SCRATCH["pk_" + _t] = ("sbuf", [128, _n], _t)
+for _k in range(8):
+    SCRATCH["ps%d" % _k] = ("psum", [128, 512], "float32")
+    _POS["ps%d" % _k] = ("ps%d" % _k, 0)
+_QUE = ("V", "S", "T", "G")
+SEMAPHORES = ["q" + e for e in _QUE] + ["ld%d" % i for i in range(12)] + ["rarr", "rloc", "st0", "st1"] + \
+    ["%s%d" % (p, t) for p in ("arr", "tarr", "loc", "tloc") for t in range(RO)]
+
+GB, EB = "SVVSVSSS", "VSVSSVSS"
+GD, ED = "SVSSVVVV", "SSVVSSSS"
+SE = "VSVSSVVV"
+
+
+def rank_program(g, core, T, topo):
+    me = T.rank_of(core)
+    if me is None:
+        return
+    others = [(me + 1 + k) % N for k in range(N - 1)]
+    ops = []
+
+    def v(name, a=None, b=None, step=1, p0=0, p1=128):
+        buf, o = _POS[name]
+        n = (_SB.get(name) or _CO.get(name) or (512, _F))[0]
+        a = 0 if a is None else a
+        b = n if b is None else b
+        return (buf, p0, p1, o + a, o + b, step)
+
+    def ap(x):
+        if x[5] == 1:
+            return T[x[0]][x[1]:x[2], x[3]:x[4]]
+        return T[x[0]][x[1]:x[2], x[3]:x[4]:x[5]]
+
+    def ncol(x):
+        return len(range(x[3], x[4], x[5]))
+
+    def arg(s):
+        return ap(s) if isinstance(s, tuple) else s
+
+    def op(q, fn, rd, wr, cost, sem=None, val=0, lag=0.06, after=None, n=1):
+        ops.append({"q": q, "fn": fn, "rd": rd, "wr": wr, "cost": cost, "sem": sem, "val": val, "lag": lag, "after": after})
+        return len(ops) - 1
+
+    cyc = 0.00083 * 1.2
+
+    def vc(n, f=1.0):
+        return 0.03 + cyc * max(64, n * f)
+
+    two = ("pk_bfloat16", "pk_float16", "pk_uint16")
+
+    def is2(x):
+        return x[0] in two or SCRATCH[x[0]][2] in (_B, _H, _U)
+
+    def tc(out, x):
+        f = 0.5 if is2(out) and is2(x) else 1.0
+        return op("V", lambda: g.vector.tensor_copy(ap(out), ap(x)), [x], [out], vc(ncol(x), f))
+
+    def tt(out, x, y, o):
+        f = 1.0 if x[0][:2] == "ps" or y[0][:2] == "ps" else 2.0
+        return op("V", lambda: g.vector.tensor_tensor(ap(out), ap(x), ap(y), o), [x, y], [out], vc(ncol(x), f))
+
+    def ts(out, x, s1, o1, s2=None, o2=None):
+        f = 0.5 if is2(out) and is2(x) else 1.0
+        rd = [x] + [s for s in (s1, s2) if isinstance(s, tuple)]
+        if o2 is None:
+            return op("V", lambda: g.vector.tensor_scalar(ap(out), ap(x), arg(s1), None, o1), rd, [out], vc(ncol(x), f))
+        return op("V", lambda: g.vector.tensor_scalar(ap(out), ap(x), arg(s1), arg(s2), o1, o2), rd, [out], vc(ncol(x), f))
+
+    def scan(out, d0, d1):
+        return op("V", lambda: g.vector.tensor_tensor_scan(ap(out), ap(d0), ap(d1), 0.0, A.mult, A.max), [d0, d1], [out], vc(ncol(d1)))
+
+    def vset(out, c):
+        return op("V", lambda: g.vector.memset(ap(out), c), [], [out], vc(ncol(out), 0.5))
+
+    def act(out, x, fn=F.Copy, bias=0.0, scale=1.0):
+        return op("S", lambda: g.scalar.activation(ap(out), ap(x), fn, bias=arg(bias), scale=arg(scale)),
+                  [x] + [s for s in (bias, scale) if isinstance(s, tuple)], [out], 0.06 + cyc * ncol(x))
+
+    def copy(q, out, x):
+        return tc(out, x) if q == "V" else act(out, x)
+
+    def gather(q, out, win, off):
+        c = 0.06 + cyc * 1.5 * ncol(out)
+        if q == "V":
+            return op("V", lambda: g.vector.tensor_copy(ap(out), ap(win).indirect(ap(off))), [win, off], [out], c)
+        return op("S", lambda: g.scalar.activation(ap(out), ap(win).indirect(ap(off)), F.Copy), [win, off], [out], c)
+
+    def gatherop(out, win, off, y, o):
+        return op("V", lambda: g.vector.tensor_tensor(ap(out), ap(win).indirect(ap(off)), ap(y), o), [win, off, y], [out],
+                  0.06 + cyc * 1.5 * ncol(out))
+
+    def scatter(win, off, x):
+        return op("V", lambda: g.vector.tensor_copy(ap(win).indirect(ap(off)), ap(x)), [x, off], [win], 0.06 + cyc * 3 * ncol(x))
+
+    def mm(out, lhsT, rhs, start=True, stop=True):
+        m = ncol(lhsT)
+        return op("T", lambda: g.tensor.matmul(ap(out), ap(lhsT), ap(rhs), start, stop), [lhsT, rhs], [out],
+                  0.0005 * max(min(64, m), ncol(rhs)))
+
+    def pick(out, x, pattern, cmp, fill, base, cm):
+        n = ncol(out)
+        return op("G", lambda: g.affine_select(ap(out), ap(x), pattern, cmp, fill, base, cm), [x], [out, pool], 0.2 + cyc * 2 * n)
+
+    def iota(out, pattern, base, cm, small=True):
+        def fn():
+            if small:
+                return g.iota(ap(out), pattern, base, cm, allow_small_or_imprecise_dtypes=True)
+            return g.iota(ap(out), pattern, base, cm)
+        return op("G", fn, [], [out, pool], 0.15 + cyc * 2 * ncol(out))
+    pool = ("pool", 0, 128, 0, 1, 1)
+
+    nld = [0]
+
+    def load(q, out, src, cost):
+        s = "ld%d" % nld[0]
+        nld[0] += 1
+        eng = g.sync if q == "D" else g.scalar
+        return op(q, lambda: eng.dma_start(ap(out), src), [], [out], 0.08, sem=s, val=16, lag=2.0 + cost)
+
+    bank = [0]
+
+    def ps(a=0, b=512, step=1, p0=0, p1=128, k=None):
+        k = bank[0] if k is None else k
+        return ("ps%d" % k, p0, p1, a, b, step)
+
+    def nb(kind=0):
+        key = kind
+        cnt[key] += 1
+        return cnt[key] % 3 if kind == 0 else 3 + cnt[key] % 5
+    cnt = {0: 0, 1: 0}
+
+    def fused(name, src, dst, sem, loc, t_lag, after=None):
+        eng = topo.engines(core, T.cores[others[0]])
+        for d in others:
+            eng = [e for e in eng if e in topo.engines(core, T.cores[d])]
+        parts, total = [eng[0:len(eng) // 4], eng[len(eng) // 4:len(eng) // 2], eng[len(eng) // 2:]], len(eng)
+
+        def fn():
+            tr = []
+            for d, es in zip(others, parts):
+                rid, pid, _ = topo.addr(T.cores[d])
+                m = 0
+                for e in es:
+                    m |= 1 << e
+                tr.append(RemoteDMATransfer(dst_ids=[DstId(rid=rid, pnc=pid)], dma_engine_mask=m, remote_sem=T.sem[sem],
+                                            srcs=[ap(src(d))], dsts=[ap(dst(d))], alu_op=0))
+            return g.remote_dma_fused(tr, local_sem=T.sem[loc])
+        return op("G", fn, [src(d) for d in others], [], 1.0, sem=loc, val=total, lag=1.5)
+
+    def got(sem, total, wr, after, lag):
+        return op("R", None, [], wr, 0.0, sem=sem, val=total, lag=lag, after=after)
+
+    def arrivals():
+        n = 0
+        for s in others:
+            od = [(s + 1 + k) % N for k in range(N - 1)]
+            eng = topo.engines(T.cores[s], T.cores[od[0]])
+            for d in od:
+                eng = [e for e in eng if e in topo.engines(T.cores[s], T.cores[d])]
+            parts = [eng[0:len(eng) // 4], eng[len(eng) // 4:len(eng) // 2], eng[len(eng) // 2:]]
+            n += len(parts[od.index(me)])
+        return n
+    narr = arrivals()
+
+    def slot(d, name, t):
+        return v("%s%d" % (name, t), DUMP + 256 * d, DUMP + 256 * d + CAP)
+
+    load("D", v("fm0"), T.fm[:], 0.5)
+    load("D", v("wk0"), T.wk[:], 0.2)
+    load("D", v("xlm", 0, W), T.lm[:], 2.0)
+    load("D", v("fr0"), T.fr[:], 3.0)
+    load("D", v("tl0"), T.tl[:], 6.0)
+    load("D", v("xmo"), T.mo[:], 9.0)
+    load("D", v("sn0"), T.sn[:], 11.0)
+    tc(v("xtl", 0, W), v("tl0"))
+    vset(v("one", 0, 128), 1.0)
+    vset(v("one", 128, 2048), 1.0)
+    o128 = v("one", 0, 128)
+    pick(v("tmp"), o128, [[-16, 8], [0, 16]], A.is_ge, 0.0, 0, 1)
+    pick(v("bo"), v("tmp"), [[16, 8], [0, 16]], A.is_ge, 0.0, 15, -1)
+    pick(v("I"), o128, [[-1, 128]], A.is_equal, 0.0, 0, 1)
+    for a in range(4):
+        pick(v("Rep", p0=32 * a, p1=32 * a + 32), v("one", 0, 512, p0=32 * a, p1=32 * a + 32), [[-1, 32], [0, 16]], A.is_equal, 0.0, 0, 1)
+    ts(v("nI"), v("I"), -1.0, A.mult)
+    tc(v("Ih"), v("I"))
+    tc(v("b8"), v("bo", 0, 128, 16))
+    ts(v("NB8"), v("b8"), -8388608.0, A.mult)
+    ts(v("PB8"), v("b8"), 131072.0, A.mult)
+    iota(v("key"), [[0, 8], [-2048, 16]], 65536 + 32768, 0)
+    iota(v("pi", 0, 1), [[0, 1]], 0, 1, False)
+    ts(v("pi", 1, 2), v("pi", 0, 1), 15, A.bitwise_and)
+    tc(v("pc", 0, 1), v("pi", 1, 2))
+    ts(v("pc", 1, 2), v("pc", 0, 1), 0.0, A.is_gt)
+    ts(v("pc", 2, 3), v("pc", 0, 1), -16.0, A.add)
+    ts(v("pc", 4, 5), v("pc", 1, 2), 65536.0, A.mult)
+    ts(v("pi", 3, 4), v("pi", 0, 1), 4, A.arith_shift_right, 1, A.bitwise_and)
+    tc(v("pc", 6, 7), v("pi", 3, 4))
+    ts(v("pc", 5, 6), v("pc", 6, 7), -1.0, A.mult, 1.0, A.add)
+    vset(v("pc", 7, 8), 1.0)
+    for k in range(4):
+        ts(v("pi", 2, 3), v("pi", 0, 1), k, A.arith_shift_right, 1, A.bitwise_and)
+        ts(v("pc", 3, 4), v("pi", 2, 3), 0.5 ** (1 << k) - 1.0, A.mult, 1.0, A.add)
+        tt(v("pc", 7, 8), v("pc", 7, 8), v("pc", 3, 4), A.mult)
+    tc(v("wkf"), v("wk0"))
+    ts(v("Wb"), v("bo"), v("wkf", 0, 1), A.mult)
+    ts(v("tri"), v("bo"), v("wkf", 1, 2), A.mult)
+    ts(v("tmp"), v("I"), v("wkf", 2, 3), A.mult)
+    b = nb(1)
+    mm(ps(0, 128, p1=24, k=b), v("one", 0, 24), v("tmp"))
+    for k in range(3):
+        pick(v("e%d" % k, p1=24), v("one", 0, 128, p1=24), [[-1, 8], [0, 16]], A.is_equal, 0.0, -8 * k, 1)
+    tt(v("ek", p1=24), v("e1", p1=24), ps(0, 128, p1=24, k=b), A.mult)
+    tt(v("EC", p1=24), v("ek", p1=24), v("e0", p1=24), A.add)
+    ts(v("ea", p1=24), v("e2", p1=24), 2048.0, A.mult)
+    tt(v("EA", p1=24), v("ea", p1=24), v("e0", p1=24), A.add)
+    vset(v("r16"), 1.0)
+    vset(v("r16", 0, 128, 16), 0.0)
+    for x in range(2):
+        w = v("wkf", x, x + 1)
+        ts(v("Wt", 8 * x, 8 * x + 8), v("b8"), w, A.mult, -1.0, A.mult)
+        b = nb(1)
+        mm(ps(0, 128, k=b), o128, v("Wb") if x == 0 else v("tri"))
+        ts(v("cT", 128 * x, 128 * x + 128), ps(0, 128, k=b), 255.0, A.mult)
+    for h in range(2):
+        tc(v("c32", h, 32, 2), v("cT", 0, 256, 16))
+    ts(v("key18"), v("key"), -65536.0, A.add, 128.0, A.mult)
+    act(v("RepN"), v("Rep"), scale=-1.0)
+    pick(v("Sel", 0, 2048, p1=8), v("one", 0, 2048, p1=8), [[-1, 16], [1, 128]], A.is_equal, 0.0, 0, -16)
+    tc(v("Selh", p1=8), v("Sel", p1=8))
+    iota(v("duT"), [[128, 2], [0, 8]], 1024, 1)
+    ts(v("dlT"), v("duT"), 1024.0, A.add)
+    for k in range(2):
+        iota(v("ti"), [[1, 1152]], 1152 * k, 0, False)
+        ts(v("tj"), v("ti"), v("pc", 7, 8), A.mult, -0.5 + 2.0 ** -12, A.add)
+        ts(v("tk"), v("tj"), 1, A.bitwise_and)
+        ts(v("tbl", 1152 * k, 1152 * k + 1152), v("tk"), 2.0, A.mult, -1.0, A.add)
+    iota(v("lane", 0, 16), [[16, 16]], 0, 0)
+    ts(v("lane", 0, 16), v("lane", 0, 16), v("pc", 0, 1), A.add)
+    ts(v("cC"), v("lane", 0, 8), 16.0, A.mult, 16.0, A.add)
+    iota(v("base"), [[256, 5], [0, 16]], 0, 0)
+    pick(v("R8", p1=8), v("one", 0, 128, p1=8), [[-1, 8], [0, 16]], A.is_equal, 0.0, 0, 1)
+    for t in range(RO - 1):
+        o = v("TR%d" % t, SL if t else 0, L)
+        act(o, v("one", 0, ncol(o)), F.Identity, 0.0, v("pc", 4, 5))
+        for d in range(N):
+            if t < RO - 2:
+                act(slot(d, "wint", t), v("one", 0, CAP), F.Identity, 0.0, v("pc", 4, 5))
+    ts(v("mkc"), v("one", 0, 512), -7.5, A.mult)
+    for a in range(2):
+        x = v("mkc", p0=64 * a, p1=64 * a + 64)
+        pick(x, x, [[0, 8], [1, 64]], A.is_gt, -100.0, 0, -1)
+    pick(v("TR"), o128, [[1, 128]], A.is_gt, 0.0, 0, -1)
+    TRI = v("TR")
+    ts(v("xsn", 0, H), v("sn0"), -1.0, A.mult, 255.0, A.add)
+
+    for s in others + [me]:
+        for t in range(RO):
+            o = v("frs", s * SL + t * CAP, s * SL + t * CAP + CAP)
+            if s == me:
+                o = slot(me, "win", t)
+            act(o, v("fr0", t * L + s * CAP, t * L + s * CAP + CAP), F.Identity, 255.0, -1.0)
+    for t in range(RO):
+        act(v("L%d" % (t + 1), SL, L), v("fr0", t * L + SL, t * L + L), F.Identity, 255.0, -1.0)
+    snd = fused("r", lambda d: v("frs", d * SL, d * SL + SL), lambda d: v("rin", me * SL, me * SL + SL), "rarr", "rloc", 0)
+    got("rarr", narr, [v("rin", s * SL, s * SL + SL) for s in others], snd, 8.0)
+    for t in range(RO):
+        for s in others:
+            act(slot(s, "win", t), v("rin", s * SL + t * CAP, s * SL + t * CAP + CAP))
+
+    ts(v("L0"), v("fm0"), -1.0, A.mult, 255.0, A.add)
+
+    def halves(name, h, n=128):
+        return v(name, h * n, h * n + n)
+
+    def todisk(b, c, X, x0, n, first, sel="Selh"):
+        for ll in range(16):
+            mm(ps(c, c + n, k=b), v(sel, 128 * ll, 128 * ll + 128, p1=8), v(X, x0 + ll, x0 + 16 * n, 16, p1=8), first and ll == 0, ll == 15)
+
+    def tolist(src, xs, out, shift):
+        b = nb(1)
+        for h in range(2):
+            mm(ps(128 * h, 128 * h + 128, p1=8, k=b), ps8(src, h), v("Ih"))
+        tc(v(xs, p1=8), ps(0, 256, p1=8, k=b))
+        b = nb(1)
+        todisk(b, 0, xs, 0, 16, True)
+        ts(v(out), ps(0, 16, k=b), shift, A.add)
+
+    def ps8(src, h):
+        return v(src, 8 * h, 8 * h + 8)
+
+    def lowest(z, q, valid):
+        tt(v("y" + z), q, valid, A.mult)
+        tt(v("V2" + z), v("y" + z), v("duT"), A.add)
+        tolist("V2" + z, "XW" + z, "WA" + z, 1024.0)
+        for k in range(2):
+            x = v("FT%d%s" % (k, z))
+            op("S", lambda x=x, k=k: g.scalar.activation(ap(x), ap(v("tbl")).indirect(ap(v("WA" + z))), F.Copy, scale=ap(v("pc", 5 + k, 6 + k))),
+               [v("tbl"), v("WA" + z), v("pc", 5 + k, 6 + k)], [x], 0.06 + cyc * 1.5 * 256)
+        for pair in range(4):
+            b, p = nb(1), 32 * pair
+            mm(ps(0, 256, k=b), v("I"), v("mkc", 0, 256), True, False)
+            for odd in range(2):
+                for lc in range(2):
+                    for blk in range(2):
+                        c, o = lc * 128 + blk * 64, (odd * 2 + lc) * 64
+                        x = v("FT%d%s" % (odd, z), c, c + 64, p0=p, p1=p + 32)
+                        mm(ps(o, o + 64, p0=64 * blk, p1=64 * blk + 64, k=b), x, x, False, False)
+            mm(ps(0, 256, k=b), v("I"), v("mkc", 0, 256), False, True)
+            act(v("SCW" + z, 256 * pair, 256 * pair + 256), ps(0, 256, k=b), F.Relu)
+        b = nb(1)
+        for lc in range(2):
+            for gr in range(8):
+                for blk in range(2):
+                    c, p = (gr * 2 + lc) * 64, 64 * blk
+                    mm(ps(lc * 8 + gr, lc * 8 + gr + 1, p0=p, p1=p + 64, k=b), v("SCW" + z, c, c + 64, p0=p, p1=p + 64),
+                       v("one", 0, 1, p0=p, p1=p + 64))
+        ts(v("nd" + z), ps(0, 16, k=b), 0.5, A.is_lt)
+        tt(v("z" + z), v("y" + z), v("nd" + z), A.mult)
+        tt(v("V3" + z), v("z" + z), v("duT"), A.add)
+        tolist("V3" + z, "XV" + z, "WL" + z, 1024.0)
+
+    for t in range(RO):
+        last = t == RO - 1
+        Lt, Ln = "L%d" % t, "L%d" % (t + 1)
+        b = nb(1)
+        for h in range(2):
+            mm(ps(h, 32, 2, k=b), halves(Lt, h), v("Wt"))
+        tt(v("au"), ps(0, 32, k=b), v("c32"), A.add)
+        ts(v("am"), v("au"), 4095, A.bitwise_and)
+        tt(v("up"), v("am", 0, 16), v("am", 16, 32), A.mult)
+        ts(v("av", 0, 16), v("up"), 5, A.arith_shift_right, 2047, A.bitwise_and)
+        ts(v("av", 16, 32), v("am", 0, 16), 2047, A.bitwise_and)
+        ts(v("av", 32, 48), v("up"), 16, A.arith_shift_right, 1, A.bitwise_and)
+        tc(v("XV"), v("av"))
+        for h in range(2):
+            act(halves("mp", h), halves(Lt, h), F.Identity, 255.0, -1.0)
+            b2 = nb(1)
+            mm(ps(0, 128, k=b2), halves("mp", h), v("I"))
+            act(halves("mT", h), ps(0, 128, k=b2))
+            b = nb(1)
+            mm(ps(0, 128, p1=24, k=b), v("XV", h, 48, 2), v("Ih"))
+            xa = v("XA", 128 * h, 128 * h + 128, p1=24)
+            tc(xa, ps(0, 128, p1=24, k=b))
+            b = nb(1)
+            mm(ps(0, 128, k=b), v("EC", p1=24), xa)
+            tc(halves("ci", h), ps(0, 128, k=b))
+            ts(halves("cj", h), halves("ci", h), 2047, A.bitwise_and)
+            tc(halves("CL", h), halves("cj", h))
+        for h in range(2):
+            for q in range(4 * h, 4 * h + 4):
+                a = q % 4
+                x, e, off = halves("X", q, 512), halves("E", q, 512), halves("CL", q, 32)
+                gather(GB[q], x, v("xlm", 0, W), off)
+                mt = v("mT", h * 128, h * 128 + 128, p0=32 * a, p1=32 * a + 32)
+                b = nb(0)
+                if EB[q] == "V":
+                    mm(ps(k=b), mt, v("Rep", p0=32 * a, p1=32 * a + 32))
+                    tt(e, x, ps(k=b), A.is_gt)
+                else:
+                    mm(ps(k=b), mt, v("RepN", p0=32 * a, p1=32 * a + 32), True, False)
+                    mm(ps(k=b), v("I"), x, False, True)
+                    act(e, ps(k=b), F.Relu)
+            b = nb(1)
+            mm(ps(0, 128, k=b), v("I"), v("key18"), True, False)
+            for i in range(16):
+                mm(ps(i, 128, 16, k=b), v("E", 2048 * h + i, 2048 * h + 2048, 16), v("NB8"), False, False)
+            mm(ps(0, 128, k=b), v("XA", 128 * h, 128 * h + 128, p1=24), v("EC", p1=24), False, True)
+            scan(halves("SC", h), v("r16"), ps(0, 128, k=b))
+            G8 = [v(z, 8 * h, 8 * h + 8) for z in ("gi", "gj", "GV", "GL")]
+            tc(G8[0], v("SC", 128 * h + 15, 128 * h + 128, 16))
+            ts(G8[1], G8[0], 2047, A.bitwise_and)
+            tc(G8[2], G8[1])
+            b = nb(1)
+            mm(ps(0, 128, p1=8, k=b), G8[2], v("Ih"))
+            tc(v("XG", 128 * h, 128 * h + 128, p1=8), ps(0, 128, p1=8, k=b))
+            b = nb(1)
+            todisk(b, 0, "XG", 128 * h, 8, True)
+            tc(G8[3], ps(0, 8, k=b))
+            gather("V", halves("TG", h), v("xtl", 0, W), G8[3])
+            gather("S", halves("xg", h), v("xlm", 0, W), G8[3])
+            b = nb(1)
+            mm(ps(0, 128, k=b), halves("xg", h), v("I"), True, False)
+            mm(ps(0, 128, k=b), halves("mp", h), v("nI"), False, True)
+            act(halves("qT", h), ps(0, 128, k=b))
+        if t < RO - 2:
+            for h in range(2):
+                x, off = halves("TGp", h), v("GL", 8 * h, 8 * h + 8)
+                op("S", lambda x=x, off=off: g.scalar.activation(ap(x), ap(v("xtl", 0, W)).indirect(ap(off)), F.Identity, bias=8192.0),
+                   [v("xtl", 0, W), off], [x], 0.06 + cyc * 1.5 * 128)
+        k15 = v("SC", 15, 256, 16)
+        ts(v("nh"), k15, 0.0, A.is_equal)
+        b = nb(1)
+        for h in range(2):
+            mm(ps(8 * h, 8 * h + 8, k=b), v("XA", 128 * h, 128 * h + 128, p1=24), v("EC", 0, 128, 16, p1=24))
+        tc(v("c0i"), ps(0, 16, k=b))
+        ts(v("c0j"), v("c0i"), 2047, A.bitwise_and)
+        tt(v("lq"), v("c0j"), v("dlT"), A.subtract)
+        lowest("l", v("lq"), v("nh"))
+        if not last:
+            b = nb(1)
+            mm(ps(0, 256, k=b), v("EA", p1=24), v("XA", p1=24))
+            b2 = nb(1)
+            act(ps(0, 256, k=b2), v("xtl", 0, L), F.Identity, 32768.0)
+            tt(v("YT"), v("TR%d" % t), ps(0, 256, k=b), A.max)
+            tt(v("CT"), v("YT"), ps(0, 256, k=b2), A.min)
+            ts(v("CTm"), v("CT"), 4095, A.bitwise_and)
+        for blk in range(3, -1, -1):
+            d = 64 * blk
+            wl = v("WLl", 4 * blk, 4 * blk + 4)
+            scatter(v("xlm"), wl, v("mp", d, d + 64))
+            if not last:
+                scatter(v("xtl"), wl, v("CTm", d, d + 64))
+        for h in range(2):
+            for q in range(4 * h, 4 * h + 4):
+                a = q % 4
+                y, p = halves("Y", q, 512), halves("P", q, 512)
+                gather(GD[q], y, v("xmo"), halves("TG", q, 32))
+                b = nb(0)
+                mm(ps(k=b), v("qT", h * 128, h * 128 + 128, p0=32 * a, p1=32 * a + 32), v("Rep", p0=32 * a, p1=32 * a + 32), True, False)
+                mm(ps(k=b), v("nI"), y, False, True)
+                if ED[q] == "V":
+                    ts(p, ps(k=b), 255.0, A.add, 0.0, A.max)
+                else:
+                    act(p, ps(k=b), F.Relu, 255.0)
+            b = nb(1)
+            for i in range(16):
+                mm(ps(i, 256, 16, k=b), v("P", 2048 * h + i, 2048 * h + 2048, 16), v("Wt"))
+            u = halves("hi", h, 256)
+            tt(u, ps(0, 256, k=b), v("cT"), A.add)
+            ts(u, u, 4095, A.bitwise_and)
+            u0, u1 = v("hi", 256 * h, 256 * h + 128), v("hi", 256 * h + 128, 256 * h + 256)
+            tt(halves("hp", h), u0, u1, A.mult)
+            ts(halves("hq", h), halves("hp", h), 5, A.arith_shift_right)
+            tt(halves("hs", h), halves("hq", h), u0, A.add)
+            ts(halves("hh", h), halves("hs", h), 2047, A.bitwise_and)
+            tc(halves("hf", h), halves("hh", h))
+            b = nb(1)
+            mm(ps(0, 128, k=b), halves("hf", h), v("Ih"))
+            tc(halves("HL", h), ps(0, 128, k=b))
+            b = nb(1)
+            mm(ps(0, 128, k=b), v("I"), v("key"), True, False)
+            mm(ps(0, 128, k=b), v("Ih"), halves("hf", h), False, True)
+            act(halves("Kh", h), ps(0, 128, k=b))
+        for h in range(2):
+            for q in range(4 * h, 4 * h + 4):
+                ne, p, sx = halves("NE", q, 512), halves("P", q, 512), halves("SX", q, 512)
+                if SE[q] == "V":
+                    gatherop(ne, v("xsn", 0, H), halves("HL", q, 32), p, A.not_equal)
+                else:
+                    gather("S", sx, v("xsn", 0, H), halves("HL", q, 32))
+                    b = nb(0)
+                    mm(ps(k=b), v("nI"), p, True, False)
+                    mm(ps(k=b), v("I"), sx, False, True)
+                    act(ne, ps(k=b), F.Abs)
+            b = nb(1)
+            for i in range(16):
+                mm(ps(i, 128, 16, k=b), v("NE", 2048 * h + i, 2048 * h + 2048, 16), v("PB8"))
+            tt(halves("k2", h), ps(0, 128, k=b), halves("Kh", h), A.min)
+            scan(halves("SC2", h), v("r16"), halves("k2", h))
+            K8 = [v(z, 8 * h, 8 * h + 8) for z in ("ki", "kj", "IV", "CHL")]
+            tc(K8[0], v("SC2", 128 * h + 15, 128 * h + 128, 16))
+            ts(K8[1], K8[0], 11, A.arith_shift_right, 31, A.bitwise_and)
+            ts(K8[2], K8[1], 1.0, A.max, -1.0, A.mult)
+            b = nb(1)
+            mm(ps(0, 128, p1=8, k=b), K8[2], v("Ih"))
+            act(v("XI", 128 * h, 128 * h + 128, p1=8), ps(0, 128, p1=8, k=b))
+            b = nb(1)
+            mm(ps(0, 8, k=b), v("I"), v("cC"), True, False)
+            todisk(b, 0, "XI", 128 * h, 8, False, "Sel")
+            tc(K8[3], ps(0, 8, k=b))
+            gather("S", halves("CH", h), halves("P", h, 2048), K8[3])
+        ts(v("has"), k15, 0.0, A.is_gt)
+        tt(v("kh"), v("SC2", 15, 256, 16), v("has"), A.mult)
+        ts(v("dd"), v("kh"), 65536 + 3, A.bitwise_and)
+        for d in range(N + 1):
+            ts(v("OH", 16 * d, 16 * d + 16), v("dd"), float(65536 + d - 1 if d else 0), A.is_equal)
+        b = nb(1)
+        mm(ps(0, 80, k=b), v("I"), v("base"), True, False)
+        for d in range(N + 1):
+            mm(ps(16 * d + 8, 16 * d + 16, k=b), o128, v("OH", 16 * d, 16 * d + 8), False, False)
+        mm(ps(0, 80, k=b), TRI, v("OH"), False, True)
+        tt(v("w3"), ps(0, 80, k=b), v("OH"), A.mult)
+        b = nb(1)
+        for h in range(2):
+            for d in range(N + 1):
+                mm(ps(128 * h, 128 * h + 128, p1=8, k=b), v("w3", 16 * d + 8 * h, 16 * d + 8 * h + 8), v("Ih"), d == 0, d == N)
+        tc(v("XS", p1=8), ps(0, 256, p1=8, k=b))
+        b = nb(1)
+        todisk(b, 0, "XS", 0, 16, True)
+        tc(v("SLL"), ps(0, 16, k=b))
+        wt = "win%d" % t
+        scatter(v(wt), v("SLL"), v("CH"))
+        mine = (me * CAP, me * CAP + CAP)
+        snd = fused("m", lambda d, t=t: slot(d, "win", t), lambda d, Ln=Ln: v(Ln, mine[0], mine[1]), "arr%d" % t, "loc%d" % t, 0)
+        act(v(Ln, mine[0], mine[1]), slot(me, "win", t))
+        got("arr%d" % t, narr, [v(Ln, s * CAP, s * CAP + CAP) for s in others], snd, 3.0)
+        if t < RO - 2:
+            TR = "TR%d" % (t + 1)
+            b = nb(1)
+            mm(ps(0, 256, k=b), v("R8", p1=8), v("XI", p1=8))
+            ts(v("mk"), ps(0, 256, k=b), v("pc", 2, 3), A.not_equal)
+            wv = v("wint%d" % t)
+            op("V", lambda wv=wv: g.vector.tensor_tensor(ap(wv).indirect(ap(v("SLL"))), ap(v("TGp")), ap(v("mk")), A.mult),
+               [v("SLL"), v("TGp"), v("mk")], [wv], 0.06 + cyc * 3 * 256)
+            snd = fused("t", lambda d, t=t: slot(d, "wint", t), lambda d, TR=TR: v(TR, mine[0], mine[1]), "tarr%d" % t, "tloc%d" % t, 0)
+            act(v(TR, mine[0], mine[1]), slot(me, "wint", t))
+            got("tarr%d" % t, narr, [v(TR, s * CAP, s * CAP + CAP) for s in others], snd, 4.0)
+        if not last:
+            ts(v("ch"), v("kh"), 2047, A.bitwise_and)
+            ts(v("nn"), v("kh"), 0.0, A.is_gt)
+            tt(v("sq"), v("ch"), v("dlT"), A.subtract)
+            lowest("s", v("sq"), v("nn"))
+            for blk in range(3, -1, -1):
+                scatter(v("xsn"), v("WLs", 4 * blk, 4 * blk + 4), v("CH", 64 * blk, 64 * blk + 64))
+    ts(v("yfo"), v("L4"), -1.0, A.mult, 255.0, A.add)
+    op("D", lambda: g.sync.dma_start(T.yf[:], ap(v("yfo"))), [v("yfo")], [], 0.08, sem="st0", val=16, lag=2.0)
+    op("D", lambda: g.sync.dma_start(T.yl[:], ap(v("xlm", 0, W))), [v("xlm", 0, W)], [], 0.08, sem="st1", val=16, lag=2.0)
+    _emit(g, T, ops)
+
+
+def _emit(g, T, ops):
+    nop = len(ops)
+    acc, deps = {}, [None] * nop
+
+    def mask(x):
+        if x[5] == 1:
+            return ((1 << (x[4] - x[3])) - 1) << x[3]
+        m = 0
+        for c in range(x[3], x[4], x[5]):
+            m |= 1 << c
+        return m
+    memo = {}
+    for i, o in enumerate(ops):
+        need = {}
+        mine = []
+        for wr, lst in ((0, o["rd"]), (1, o["wr"])):
+            for x in lst:
+                if x not in memo:
+                    memo[x] = mask(x)
+                mine.append((x[0], x[1], x[2], memo[x], wr))
+        for (bf, p0, p1, m, wr) in mine:
+            for (j, q0, q1, mj, wj) in acc.get(bf, ()):
+                if j == i:
+                    continue
+                same = ops[j]["q"] == o["q"]
+                if bf[:2] == "ps":
+                    hit = not same or ((wr or wj) and (m & mj) and p0 < q1 and q0 < p1)
+                else:
+                    hit = (wr or wj) and (m & mj) and p0 < q1 and q0 < p1
+                if not hit and bf[:2] == "ps":
+                    need[j] = max(need.get(j, 0), 1)
+                if hit:
+                    k = 2
+                    if same and o["q"] == "T":
+                        k = 1
+                    need[j] = max(need.get(j, 0), k)
+        for (bf, p0, p1, m, wr) in mine:
+            old = acc.get(bf, [])
+            if bf[:2] == "ps":
+                old = [z for z in old if z[0] == i]
+            elif wr:
+                old = [z for z in old if not (z[0] != i and (z[3] | m) == m and p0 <= z[1] and z[2] <= p1)]
+            acc[bf] = old + [(i, p0, p1, m, wr)]
+        if o["after"] is not None:
+            need[o["after"]] = max(need.get(o["after"], 0), 1)
+        deps[i] = need
+    tail = [0.0] * nop
+    succ = [[] for _ in range(nop)]
+    for i in range(nop):
+        for j in deps[i]:
+            succ[j].append(i)
+    for i in range(nop - 1, -1, -1):
+        o = ops[i]
+        tail[i] = o["cost"] + max([tail[j] + o["lag"] for j in succ[i]] + [0.0])
+    left = [len(d) for d in deps]
+    est = [0.0] * nop
+    ready = {}
+    for i in range(nop):
+        if left[i] == 0:
+            ready.setdefault(ops[i]["q"], []).append(i)
+    clock, order, done = {}, [], 0
+    while done < nop:
+        best = None
+        for q, lst in ready.items():
+            if not lst:
+                continue
+            c = clock.get(q, 0.0)
+            s = max(c, min(est[i] for i in lst)) if q != "R" else min(est[i] for i in lst)
+            if best is None or s < best[0]:
+                best = (s, q)
+        s, q = best
+        i = max([z for z in ready[q] if est[z] <= s + 1e-9], key=lambda z: (tail[z], -z))
+        ready[q].remove(i)
+        o = ops[i]
+        if q != "R":
+            clock[q] = s + o["cost"]
+        order.append(i)
+        done += 1
+        for j in succ[i]:
+            e = s + o["cost"] + (o["lag"] if q != "R" and (deps[j][i] == 2 or q == "G") else 0.0)
+            if ops[j]["q"] == "R":
+                e = s + o["cost"] + ops[j]["lag"]
+            est[j] = max(est[j], e)
+            left[j] -= 1
+            if left[j] == 0:
+                ready.setdefault(ops[j]["q"], []).append(j)
+    queue = {"V": g.vector, "S": g.scalar, "T": g.tensor, "G": g, "D": g.sync}
+    count = {}
+    know = {q: {} for q in queue}
+    tok, kn = [None] * nop, [None] * nop
+    for i in order:
+        o = ops[i]
+        q = o["q"]
+        if q == "R":
+            tok[i] = (o["sem"], o["val"])
+            kn[i] = {o["sem"]: o["val"]}
+            continue
+        k = know[q]
+        want = {}
+        for j, kind in deps[i].items():
+            if kind == 2:
+                s, val = tok[j]
+                if k.get(s, 0) < val and (s not in want or want[s][0] < val):
+                    want[s] = (val, j)
+        for s in list(want):
+            if any(z != s and kn[want[z][1]].get(s, 0) >= want[s][0] for z in want):
+                del want[s]
+        for s, (val, j) in want.items():
+            queue[q].wait_ge(T.sem[s], val)
+        for s, (val, j) in want.items():
+            for z, n in kn[j].items():
+                if k.get(z, 0) < n:
+                    k[z] = n
+        ins = o["fn"]()
+        if o["sem"] is None:
+            s = "q" + q
+            count[s] = count.get(s, 0) + 1
+            ins.then_inc(T.sem[s], 1)
+            tok[i] = (s, count[s])
+        else:
+            tok[i] = (o["sem"], o["val"])
+            if q == "D":
+                ins.then_inc(T.sem[o["sem"]], 16)
+        kn[i] = dict(k)
+        kn[i][tok[i][0]] = tok[i][1]
+    k = know["G"]
+    fin = {}
+    for i in range(nop):
+        if tok[i][1] > fin.get(tok[i][0], 0):
+            fin[tok[i][0]] = tok[i][1]
+    for s, n in fin.items():
+        if k.get(s, 0) < n:
+            g.wait_ge(T.sem[s], n)

@@ -11,7 +11,7 @@ _SB = {
     "wint0": (SW, _F), "wint1": (SW, _F),
     "L0": (L, _B), "L1": (L, _B), "L2": (L, _B), "L3": (L, _B), "L4": (L, _B), "TR0": (L, _F), "TR1": (L, _F), "TR2": (L, _F), "yfo": (L, _B),
     "mp": (L, _B), "mT": (L, _B), "qT": (L, _B), "au": (32, _I), "am": (32, _I), "up": (16, _I), "av": (48, _I), "ci": (L, _I),
-    "cj": (L, _I), "XV": (48, _H), "XA": (256, _H), "tl0": (W, _I), "ti": (1152, _I), "tj": (1152, _I), "tk": (1152, _I), "tbl": (2304, _B),
+    "cj": (L, _I), "XV": (48, _H), "XA": (256, _H), "tl0": (W, _I), "ti": (12, _F), "tj": (12, _F), "tk": (12, _F), "tbl": (2304, _B),
     "CL": (L, _U), "X": (4096, _B), "E": (4096, _B), "Y": (4096, _B), "P": (4096, _B), "NE": (4096, _B), "SX": (4096, _B),
     "SC": (256, _F), "gi": (16, _I), "gj": (16, _I), "GV": (16, _H), "XG": (256, _H), "GL": (16, _U), "TG": (L, _U), "xg": (L, _B),
     "hi": (512, _I), "hp": (256, _I), "hq": (256, _I), "hs": (256, _I), "hh": (256, _I), "hf": (256, _H), "HL": (256, _U), "Kh": (256, _F),
@@ -26,10 +26,10 @@ for _z in "ls":
                    "z": (16, _F), "V3": (16, _H), "XV": (256, _H), "WL": (16, _U)}.items():
         _SB[_k + _z] = _v
 _CO = {
-    "one": (2048, _B), "I": (128, _B), "nI": (128, _B), "Ih": (128, _H), "bo": (128, _B), "b8": (8, _B), "tmp": (128, _B), "tri": (128, _B),
-    "Rep": (512, _B), "RepN": (512, _B), "Sel": (2048, _B), "Selh": (2048, _H), "R8": (128, _B), "TR": (128, _B), "key": (128, _B),
+    "one": (512, _B), "I": (128, _B), "nI": (128, _B), "Ih": (128, _H), "bo": (128, _B), "b8": (8, _B), "tmp": (128, _B), "tri": (128, _B),
+    "Rep": (512, _B), "RepN": (512, _B), "Sel": (144, _B), "Selh": (144, _H), "i4": (128, _B), "R8": (128, _B), "TR": (128, _B), "key": (128, _B),
     "key18": (128, _B), "r16": (128, _F), "cC": (8, _B), "lane": (16, _F), "base": (80, _B),
-    "mkc": (512, _B), "pc": (8, _F), "pi": (4, _I), "Wb": (128, _B), "Wt": (16, _B), "cT": (256, _F), "NB8": (8, _B), "PB8": (8, _B),
+    "mkc": (256, _B), "pc": (8, _F), "pi": (4, _I), "Wb": (128, _B), "Wt": (16, _B), "cT": (256, _F), "NB8": (8, _B), "PB8": (8, _B),
     "c32": (32, _F), "duT": (16, _F), "dlT": (16, _F), "e0": (128, _F), "e1": (128, _F), "e2": (128, _F), "ek": (128, _F), "ea": (128, _F),
     "EC": (128, _H), "EA": (128, _H),
 }
@@ -224,13 +224,20 @@ def rank_program(g, core, T, topo):
     load("D", v("sn0"), T.sn[:], 11.0)
     tc(v("xtl", 0, W), v("tl0"))
     vset(v("one", 0, 128), 1.0)
-    vset(v("one", 128, 2048), 1.0)
+    vset(v("one", 128, 512), 1.0)
     o128 = v("one", 0, 128)
+    pick(v("I"), o128, [[-1, 128]], A.is_equal, 0.0, 0, 1)
     pick(v("tmp"), o128, [[-16, 8], [0, 16]], A.is_ge, 0.0, 0, 1)
     pick(v("bo"), v("tmp"), [[16, 8], [0, 16]], A.is_ge, 0.0, 15, -1)
-    pick(v("I"), o128, [[-1, 128]], A.is_equal, 0.0, 0, 1)
+    for k in range(3):
+        pick(v("e%d" % k, p1=24), v("one", 0, 128, p1=24), [[-1, 8], [0, 16]], A.is_equal, 0.0, -8 * k, 1)
+    pick(v("RepN", p1=32), v("one", 0, 512, p1=32), [[-1, 32], [0, 16]], A.is_equal, 0.0, 0, 1)
     for a in range(4):
-        pick(v("Rep", p0=32 * a, p1=32 * a + 32), v("one", 0, 512, p0=32 * a, p1=32 * a + 32), [[-1, 32], [0, 16]], A.is_equal, 0.0, 0, 1)
+        act(v("i4", 32 * a, 32 * a + 32, p1=32), v("I", 0, 32, p1=32))
+    b = nb(0)
+    mm(ps(k=b), v("i4", p1=32), v("RepN", p1=32))
+    act(v("Rep"), ps(k=b))
+    act(v("RepN"), ps(k=b), scale=-1.0)
     ts(v("nI"), v("I"), -1.0, A.mult)
     tc(v("Ih"), v("I"))
     tc(v("b8"), v("bo", 0, 128, 16))
@@ -246,19 +253,12 @@ def rank_program(g, core, T, topo):
     ts(v("pi", 3, 4), v("pi", 0, 1), 4, A.arith_shift_right, 1, A.bitwise_and)
     tc(v("pc", 6, 7), v("pi", 3, 4))
     ts(v("pc", 5, 6), v("pc", 6, 7), -1.0, A.mult, 1.0, A.add)
-    vset(v("pc", 7, 8), 1.0)
-    for k in range(4):
-        ts(v("pi", 2, 3), v("pi", 0, 1), k, A.arith_shift_right, 1, A.bitwise_and)
-        ts(v("pc", 3, 4), v("pi", 2, 3), 0.5 ** (1 << k) - 1.0, A.mult, 1.0, A.add)
-        tt(v("pc", 7, 8), v("pc", 7, 8), v("pc", 3, 4), A.mult)
     tc(v("wkf"), v("wk0"))
     ts(v("Wb"), v("bo"), v("wkf", 0, 1), A.mult)
     ts(v("tri"), v("bo"), v("wkf", 1, 2), A.mult)
     ts(v("tmp"), v("I"), v("wkf", 2, 3), A.mult)
     b = nb(1)
     mm(ps(0, 128, p1=24, k=b), v("one", 0, 24), v("tmp"))
-    for k in range(3):
-        pick(v("e%d" % k, p1=24), v("one", 0, 128, p1=24), [[-1, 8], [0, 16]], A.is_equal, 0.0, -8 * k, 1)
     tt(v("ek", p1=24), v("e1", p1=24), ps(0, 128, p1=24, k=b), A.mult)
     tt(v("EC", p1=24), v("ek", p1=24), v("e0", p1=24), A.add)
     ts(v("ea", p1=24), v("e2", p1=24), 2048.0, A.mult)
@@ -271,19 +271,22 @@ def rank_program(g, core, T, topo):
         b = nb(1)
         mm(ps(0, 128, k=b), o128, v("Wb") if x == 0 else v("tri"))
         ts(v("cT", 128 * x, 128 * x + 128), ps(0, 128, k=b), 255.0, A.mult)
+    b = nb(1)
+    mm(ps(0, 16, k=b), o128, v("Wt"))
     for h in range(2):
-        tc(v("c32", h, 32, 2), v("cT", 0, 256, 16))
+        ts(v("c32", h, 32, 2), ps(0, 16, k=b), -255.0, A.mult)
     ts(v("key18"), v("key"), -65536.0, A.add, 128.0, A.mult)
-    act(v("RepN"), v("Rep"), scale=-1.0)
-    pick(v("Sel", 0, 2048, p1=8), v("one", 0, 2048, p1=8), [[-1, 16], [1, 128]], A.is_equal, 0.0, 0, -16)
+    pick(v("Sel", p1=8), v("one", 0, 144, p1=8), [[1, 144]], A.is_equal, 0.0, -16, -16)
     tc(v("Selh", p1=8), v("Sel", p1=8))
     iota(v("duT"), [[128, 2], [0, 8]], 1024, 1)
     ts(v("dlT"), v("duT"), 1024.0, A.add)
-    for k in range(2):
-        iota(v("ti"), [[1, 1152]], 1152 * k, 0, False)
-        ts(v("tj"), v("ti"), v("pc", 7, 8), A.mult, -0.5 + 2.0 ** -12, A.add)
-        ts(v("tk"), v("tj"), 1, A.bitwise_and)
-        ts(v("tbl", 1152 * k, 1152 * k + 1152), v("tk"), 2.0, A.mult, -1.0, A.add)
+    iota(v("ti"), [[1, 12]], 0, 0)
+    ts(v("tj"), v("ti"), v("pc", 0, 1), A.is_equal)
+    ts(v("tk"), v("tj"), 2.0, A.mult, -1.0, A.add)
+    vset(v("tbl", 0, 1), -1.0)
+    for k in range(12):
+        n = min(1 << k, 2304 - (1 << k))
+        ts(v("tbl", 1 << k, (1 << k) + n), v("tbl", 0, n), v("tk", k, k + 1), A.max)
     iota(v("lane", 0, 16), [[16, 16]], 0, 0)
     ts(v("lane", 0, 16), v("lane", 0, 16), v("pc", 0, 1), A.add)
     ts(v("cC"), v("lane", 0, 8), 16.0, A.mult, 16.0, A.add)
@@ -295,10 +298,10 @@ def rank_program(g, core, T, topo):
         for d in range(N):
             if t < RO - 2:
                 act(slot(d, "wint", t), v("one", 0, CAP), F.Identity, 0.0, v("pc", 4, 5))
-    ts(v("mkc"), v("one", 0, 512), -7.5, A.mult)
+    ts(v("mkc"), v("one", 0, 256), -7.5, A.mult)
     for a in range(2):
         x = v("mkc", p0=64 * a, p1=64 * a + 64)
-        pick(x, x, [[0, 8], [1, 64]], A.is_gt, -100.0, 0, -1)
+        pick(x, x, [[0, 4], [1, 64]], A.is_gt, -100.0, 0, -1)
     pick(v("TR"), o128, [[1, 128]], A.is_gt, 0.0, 0, -1)
     TRI = v("TR")
     ts(v("xsn", 0, H), v("sn0"), -1.0, A.mult, 255.0, A.add)
@@ -324,7 +327,7 @@ def rank_program(g, core, T, topo):
 
     def todisk(b, c, X, x0, n, first, sel="Selh"):
         for ll in range(16):
-            mm(ps(c, c + n, k=b), v(sel, 128 * ll, 128 * ll + 128, p1=8), v(X, x0 + ll, x0 + 16 * n, 16, p1=8), first and ll == 0, ll == 15)
+            mm(ps(c, c + n, k=b), v(sel, 16 - ll, 144 - ll, p1=8), v(X, x0 + ll, x0 + 16 * n, 16, p1=8), first and ll == 0, ll == 15)
 
     def tolist(src, xs, out, shift):
         b = nb(1)

@@ -11,25 +11,25 @@ _SB = {
     "wint0": (SW, _F), "wint1": (SW, _F),
     "L0": (L, _B), "L1": (L, _B), "L2": (L, _B), "L3": (L, _B), "L4": (L, _B), "TR0": (L, _F), "TR1": (L, _F), "TR2": (L, _F), "yfo": (L, _B),
     "mp": (L, _B), "mT": (L, _B), "qT": (L, _B), "au": (32, _I), "am": (32, _I), "up": (16, _I), "av": (48, _I), "ci": (L, _I),
-    "cj": (L, _I), "XV": (48, _H), "XA": (256, _H), "tl0": (W, _I), "ti": (12, _F), "tj": (12, _F), "tk": (12, _F), "tbl": (2304, _B),
+    "cj": (L, _I), "XV": (48, _H), "XA": (256, _H), "ti": (12, _F), "tj": (12, _F), "tk": (12, _F), "tbl": (2304, _B),
     "CL": (L, _U), "X": (4096, _B), "E": (4096, _B), "Y": (4096, _B), "P": (4096, _B), "NE": (4096, _B), "SX": (4096, _B),
-    "SC": (256, _F), "gi": (16, _I), "gj": (16, _I), "GV": (16, _H), "XG": (256, _H), "GL": (16, _U), "TG": (L, _U), "xg": (L, _B),
+    "SC": (272, _F), "gi": (16, _I), "gj": (16, _I), "GV": (16, _H), "XG": (256, _H), "GL": (16, _U), "TG": (L, _U), "xg": (L, _B),
     "hi": (512, _I), "hp": (256, _I), "hq": (256, _I), "hs": (256, _I), "hh": (256, _I), "hf": (256, _H), "HL": (256, _U), "Kh": (256, _F),
     "k2": (256, _F), "SC2": (256, _F), "ki": (16, _I), "kj": (16, _I), "IV": (16, _H), "XI": (256, _B), "CHL": (16, _U), "CH": (L, _B),
     "has": (16, _F), "kh": (16, _I), "ch": (16, _I), "cd": (16, _I), "nc": (16, _I), "dd": (16, _I), "OH": (80, _B),
     "w3": (80, _H), "rin": (N * SL, _B), "XS": (256, _H), "sf": (16, _F), "SLL": (16, _U),
     "TGp": (L, _F), "mk": (L, _F), "YT": (L, _F), "CT": (L, _I), "CTm": (L, _I),
-    "nh": (16, _F), "nn": (16, _F), "c0i": (16, _I), "c0j": (16, _I), "lq": (16, _F), "sq": (16, _F),
+    "nh": (16, _B), "nn": (16, _B), "lq": (16, _F), "sq": (16, _F),
 }
 for _z in "ls":
-    for _k, _v in {"y": (16, _F), "V2": (16, _H), "XW": (256, _H), "WA": (16, _U), "FT0": (L, _B), "FT1": (L, _B), "SCW": (1024, _B), "nd": (16, _F),
+    for _k, _v in {"y": (16, _F), "V2": (16, _H), "XW": (256, _H), "WA": (16, _U), "FT0": (L, _B), "FT1": (L, _B), "SCW": (1024, _B), "SCM": (1024, _B), "nd": (16, _F),
                    "z": (16, _F), "V3": (16, _H), "XV": (256, _H), "WL": (16, _U)}.items():
         _SB[_k + _z] = _v
 _CO = {
     "one": (512, _B), "I": (128, _B), "nI": (128, _B), "Ih": (128, _H), "bo": (128, _B), "b8": (8, _B), "tmp": (128, _B), "tri": (128, _B),
     "Rep": (512, _B), "RepN": (512, _B), "Sel": (144, _B), "Selh": (144, _H), "i4": (128, _B), "R8": (128, _B), "TR": (128, _B), "key": (128, _B),
-    "key18": (128, _B), "r16": (128, _F), "cC": (8, _B), "lane": (16, _F), "base": (80, _B),
-    "mkc": (256, _B), "pc": (8, _F), "pi": (4, _I), "Wb": (128, _B), "Wt": (16, _B), "cT": (256, _F), "NB8": (8, _B), "PB8": (8, _B),
+    "key18": (136, _B), "r16": (128, _F), "cC": (16, _B), "lane": (16, _F), "base": (80, _B),
+    "i5": (40, _B), "mkc": (256, _B), "EC17": (136, _H), "key17": (136, _B), "r17": (136, _F), "pc": (8, _F), "pi": (4, _I), "Wb": (128, _B), "Wt": (16, _B), "cT": (256, _F), "NB8": (8, _B), "PB8": (8, _B),
     "c32": (32, _F), "duT": (16, _F), "dlT": (16, _F), "e0": (128, _F), "e1": (128, _F), "e2": (128, _F), "ek": (128, _F), "ea": (128, _F),
     "EC": (128, _H), "EA": (128, _H),
 }
@@ -57,9 +57,10 @@ _QUE = ("V", "S", "T", "G")
 SEMAPHORES = ["q" + e for e in _QUE] + ["ld%d" % i for i in range(12)] + ["rarr", "rloc", "st0", "st1"] + \
     ["%s%d" % (p, t) for p in ("arr", "tarr", "loc", "tloc") for t in range(RO)]
 
-GB, EB = "SVVSVSSS", "VSVSSVSS"
-GD, ED = "SVSSVVVV", "SSVVSSSS"
-SE = "VSVSSVVV"
+GB, EB = "VSSSVVSS", "VVVVSSVS"
+GD, ED = "SVSSVSSV", "VSSVSSSV"
+SE = "SSVSSVVV"
+BI = (-11.0, -8.0, -2.0, -1.0)
 
 
 def rank_program(g, core, T, topo):
@@ -68,6 +69,7 @@ def rank_program(g, core, T, topo):
         return
     others = [(me + 1 + k) % N for k in range(N - 1)]
     ops = []
+    bias = [0.0]
 
     def v(name, a=None, b=None, step=1, p0=0, p1=128):
         buf, o = _POS[name]
@@ -88,7 +90,7 @@ def rank_program(g, core, T, topo):
         return ap(s) if isinstance(s, tuple) else s
 
     def op(q, fn, rd, wr, cost, sem=None, val=0, lag=0.06, after=None, n=1):
-        ops.append({"q": q, "fn": fn, "rd": rd, "wr": wr, "cost": cost, "sem": sem, "val": val, "lag": lag, "after": after})
+        ops.append({"q": q, "fn": fn, "rd": rd, "wr": wr, "cost": cost, "sem": sem, "val": val, "lag": lag, "after": after, "bias": bias[0]})
         return len(ops) - 1
 
     cyc = 0.00083 * 1.2
@@ -165,7 +167,7 @@ def rank_program(g, core, T, topo):
         s = "ld%d" % nld[0]
         nld[0] += 1
         eng = g.sync if q == "D" else g.scalar
-        return op(q, lambda: eng.dma_start(ap(out), src), [], [out], 0.08, sem=s, val=16, lag=2.0 + cost)
+        return op(q, lambda: eng.dma_start(ap(out), src), [], [out, ("order", 0, 128, 0, 1, 2)], 0.08, sem=s, val=16, lag=2.0 + cost)
 
     bank = [0]
 
@@ -174,10 +176,9 @@ def rank_program(g, core, T, topo):
         return ("ps%d" % k, p0, p1, a, b, step)
 
     def nb(kind=0):
-        key = kind
-        cnt[key] += 1
-        return cnt[key] % 3 if kind == 0 else 3 + cnt[key] % 5
-    cnt = {0: 0, 1: 0}
+        cnt[kind] += 1
+        return (cnt[kind] % 2, 2 + cnt[kind] % 4, 6 + cnt[kind] % 2)[kind]
+    cnt = {0: 0, 1: 0, 2: 0}
 
     def fused(name, src, dst, sem, loc, t_lag, after=None):
         eng = topo.engines(core, T.cores[others[0]])
@@ -218,11 +219,10 @@ def rank_program(g, core, T, topo):
     load("D", v("fm0"), T.fm[:], 0.5)
     load("D", v("wk0"), T.wk[:], 0.2)
     load("D", v("xlm", 0, W), T.lm[:], 2.0)
-    load("D", v("fr0"), T.fr[:], 3.0)
-    load("D", v("tl0"), T.tl[:], 6.0)
-    load("D", v("xmo"), T.mo[:], 9.0)
+    load("D", v("xtl", 0, W), T.tl[:], 5.0)
+    load("D", v("xmo"), T.mo[:], 8.0)
+    load("D", v("fr0"), T.fr[:], 9.0)
     load("D", v("sn0"), T.sn[:], 11.0)
-    tc(v("xtl", 0, W), v("tl0"))
     vset(v("one", 0, 128), 1.0)
     vset(v("one", 128, 512), 1.0)
     o128 = v("one", 0, 128)
@@ -275,10 +275,20 @@ def rank_program(g, core, T, topo):
     mm(ps(0, 16, k=b), o128, v("Wt"))
     for h in range(2):
         ts(v("c32", h, 32, 2), ps(0, 16, k=b), -255.0, A.mult)
-    ts(v("key18"), v("key"), -65536.0, A.add, 128.0, A.mult)
+    for gr in range(8):
+        tc(v("EC17", 17 * gr, 17 * gr + 16, p1=24), v("EC", 16 * gr, 16 * gr + 16, p1=24))
+    tc(v("EC17", 16, 136, 17, p1=24), v("EC", 0, 128, 16, p1=24))
+    iota(v("key17"), [[0, 8], [-2048, 17]], 32768, 0)
+    ts(v("key18"), v("key17"), 128.0, A.mult)
+    vset(v("r17"), 1.0)
+    vset(v("r17", 0, 136, 17), 0.0)
     pick(v("Sel", p1=8), v("one", 0, 144, p1=8), [[1, 144]], A.is_equal, 0.0, -16, -16)
-    tc(v("Selh", p1=8), v("Sel", p1=8))
-    iota(v("duT"), [[128, 2], [0, 8]], 1024, 1)
+    for k in range(5):
+        act(v("i5", 8 * k, 8 * k + 8, p1=8), v("I", 0, 8, p1=8))
+    b = nb(1)
+    mm(ps(0, 144, p1=40, k=b), v("i5", p1=8), v("Sel", p1=8))
+    tc(v("Selh", p1=40), ps(0, 144, p1=40, k=b))
+    iota(v("duT"), [[0, 8], [128, 2]], 1024, 1)
     ts(v("dlT"), v("duT"), 1024.0, A.add)
     iota(v("ti"), [[1, 12]], 0, 0)
     ts(v("tj"), v("ti"), v("pc", 0, 1), A.is_equal)
@@ -289,7 +299,8 @@ def rank_program(g, core, T, topo):
         ts(v("tbl", 1 << k, (1 << k) + n), v("tbl", 0, n), v("tk", k, k + 1), A.max)
     iota(v("lane", 0, 16), [[16, 16]], 0, 0)
     ts(v("lane", 0, 16), v("lane", 0, 16), v("pc", 0, 1), A.add)
-    ts(v("cC"), v("lane", 0, 8), 16.0, A.mult, 16.0, A.add)
+    for h in range(2):
+        ts(v("cC", 8 * h, 8 * h + 8), v("lane", 0, 8), 16.0, A.mult, 16.0, A.add)
     iota(v("base"), [[256, 5], [0, 16]], 0, 0)
     pick(v("R8", p1=8), v("one", 0, 128, p1=8), [[-1, 8], [0, 16]], A.is_equal, 0.0, 0, 1)
     for t in range(RO - 1):
@@ -298,11 +309,11 @@ def rank_program(g, core, T, topo):
         for d in range(N):
             if t < RO - 2:
                 act(slot(d, "wint", t), v("one", 0, CAP), F.Identity, 0.0, v("pc", 4, 5))
+    pick(v("TR"), o128, [[1, 128]], A.is_gt, 0.0, 0, -1)
     ts(v("mkc"), v("one", 0, 256), -7.5, A.mult)
     for a in range(2):
         x = v("mkc", p0=64 * a, p1=64 * a + 64)
         pick(x, x, [[0, 4], [1, 64]], A.is_gt, -100.0, 0, -1)
-    pick(v("TR"), o128, [[1, 128]], A.is_gt, 0.0, 0, -1)
     TRI = v("TR")
     ts(v("xsn", 0, H), v("sn0"), -1.0, A.mult, 255.0, A.add)
 
@@ -325,48 +336,45 @@ def rank_program(g, core, T, topo):
     def halves(name, h, n=128):
         return v(name, h * n, h * n + n)
 
-    def todisk(b, c, X, x0, n, first, sel="Selh"):
+    def todisk(b, c, X, x0, n, first, sel="Selh", rows=8):
         for ll in range(16):
-            mm(ps(c, c + n, k=b), v(sel, 16 - ll, 144 - ll, p1=8), v(X, x0 + ll, x0 + 16 * n, 16, p1=8), first and ll == 0, ll == 15)
+            mm(ps(c, c + n, k=b), v(sel, 16 - ll, 144 - ll, p1=rows), v(X, x0 + ll, x0 + 16 * n, 16, p1=rows), first and ll == 0, ll == 15)
 
     def tolist(src, xs, out, shift):
-        b = nb(1)
+        b = nb(2)
         for h in range(2):
             mm(ps(128 * h, 128 * h + 128, p1=8, k=b), ps8(src, h), v("Ih"))
         tc(v(xs, p1=8), ps(0, 256, p1=8, k=b))
-        b = nb(1)
+        b = nb(2)
         todisk(b, 0, xs, 0, 16, True)
         ts(v(out), ps(0, 16, k=b), shift, A.add)
 
     def ps8(src, h):
-        return v(src, 8 * h, 8 * h + 8)
+        return v(src, h, 16, 2)
 
-    def lowest(z, q, valid):
-        tt(v("y" + z), q, valid, A.mult)
-        tt(v("V2" + z), v("y" + z), v("duT"), A.add)
-        tolist("V2" + z, "XW" + z, "WA" + z, 1024.0)
+    def lowest(z, places, q, valid):
         for k in range(2):
             x = v("FT%d%s" % (k, z))
-            op("S", lambda x=x, k=k: g.scalar.activation(ap(x), ap(v("tbl")).indirect(ap(v("WA" + z))), F.Copy, scale=ap(v("pc", 5 + k, 6 + k))),
-               [v("tbl"), v("WA" + z), v("pc", 5 + k, 6 + k)], [x], 0.06 + cyc * 1.5 * 256)
+            op("S", lambda x=x, k=k: g.scalar.activation(ap(x), ap(v("tbl")).indirect(ap(v(places))), F.Copy, scale=ap(v("pc", 5 + k, 6 + k))),
+               [v("tbl"), v(places), v("pc", 5 + k, 6 + k)], [x], 0.06 + cyc * 1.5 * 256)
+        tt(v("y" + z), q, valid, A.mult)
         for pair in range(4):
-            b, p = nb(1), 32 * pair
-            mm(ps(0, 256, k=b), v("I"), v("mkc", 0, 256), True, False)
+            b, p = nb(2), 32 * pair
+            mm(ps(0, 256, k=b), v("I"), v("mkc"), True, False)
             for odd in range(2):
                 for lc in range(2):
                     for blk in range(2):
                         c, o = lc * 128 + blk * 64, (odd * 2 + lc) * 64
                         x = v("FT%d%s" % (odd, z), c, c + 64, p0=p, p1=p + 32)
                         mm(ps(o, o + 64, p0=64 * blk, p1=64 * blk + 64, k=b), x, x, False, False)
-            mm(ps(0, 256, k=b), v("I"), v("mkc", 0, 256), False, True)
+            mm(ps(0, 256, k=b), v("I"), v("mkc"), False, True)
             act(v("SCW" + z, 256 * pair, 256 * pair + 256), ps(0, 256, k=b), F.Relu)
-        b = nb(1)
-        for lc in range(2):
-            for gr in range(8):
-                for blk in range(2):
-                    c, p = (gr * 2 + lc) * 64, 64 * blk
-                    mm(ps(lc * 8 + gr, lc * 8 + gr + 1, p0=p, p1=p + 64, k=b), v("SCW" + z, c, c + 64, p0=p, p1=p + 64),
-                       v("one", 0, 1, p0=p, p1=p + 64))
+        b = nb(2)
+        for k in range(16):
+            for blk in range(2):
+                p = 64 * blk
+                mm(ps(k, k + 1, p0=p, p1=p + 64, k=b), v("SCW" + z, 64 * k, 64 * k + 64, p0=p, p1=p + 64),
+                   (valid[0], p, p + 64, valid[3] + k, valid[3] + k + 1, 1))
         ts(v("nd" + z), ps(0, 16, k=b), 0.5, A.is_lt)
         tt(v("z" + z), v("y" + z), v("nd" + z), A.mult)
         tt(v("V3" + z), v("z" + z), v("duT"), A.add)
@@ -375,6 +383,7 @@ def rank_program(g, core, T, topo):
     for t in range(RO):
         last = t == RO - 1
         Lt, Ln = "L%d" % t, "L%d" % (t + 1)
+        bias[0] = 0.0
         b = nb(1)
         for h in range(2):
             mm(ps(h, 32, 2, k=b), halves(Lt, h), v("Wt"))
@@ -414,13 +423,13 @@ def rank_program(g, core, T, topo):
                     mm(ps(k=b), v("I"), x, False, True)
                     act(e, ps(k=b), F.Relu)
             b = nb(1)
-            mm(ps(0, 128, k=b), v("I"), v("key18"), True, False)
+            mm(ps(0, 136, k=b), v("I"), v("key18"), True, False)
             for i in range(16):
-                mm(ps(i, 128, 16, k=b), v("E", 2048 * h + i, 2048 * h + 2048, 16), v("NB8"), False, False)
-            mm(ps(0, 128, k=b), v("XA", 128 * h, 128 * h + 128, p1=24), v("EC", p1=24), False, True)
-            scan(halves("SC", h), v("r16"), ps(0, 128, k=b))
+                mm(ps(i, 136, 17, k=b), v("E", 2048 * h + i, 2048 * h + 2048, 16), v("NB8"), False, False)
+            mm(ps(0, 136, k=b), v("XA", 128 * h, 128 * h + 128, p1=24), v("EC17", p1=24), False, True)
+            scan(halves("SC", h, 136), v("r17"), ps(0, 136, k=b))
             G8 = [v(z, 8 * h, 8 * h + 8) for z in ("gi", "gj", "GV", "GL")]
-            tc(G8[0], v("SC", 128 * h + 15, 128 * h + 128, 16))
+            tc(G8[0], v("SC", 136 * h + 16, 136 * h + 136, 17))
             ts(G8[1], G8[0], 2047, A.bitwise_and)
             tc(G8[2], G8[1])
             b = nb(1)
@@ -436,24 +445,19 @@ def rank_program(g, core, T, topo):
             mm(ps(0, 128, k=b), halves("mp", h), v("nI"), False, True)
             act(halves("qT", h), ps(0, 128, k=b))
         if t < RO - 2:
-            for h in range(2):
-                x, off = halves("TGp", h), v("GL", 8 * h, 8 * h + 8)
-                op("S", lambda x=x, off=off: g.scalar.activation(ap(x), ap(v("xtl", 0, W)).indirect(ap(off)), F.Identity, bias=8192.0),
-                   [v("xtl", 0, W), off], [x], 0.06 + cyc * 1.5 * 128)
-        k15 = v("SC", 15, 256, 16)
-        ts(v("nh"), k15, 0.0, A.is_equal)
-        b = nb(1)
+            ts(v("TGp"), v("TG"), 8192.0, A.add)
         for h in range(2):
-            mm(ps(8 * h, 8 * h + 8, k=b), v("XA", 128 * h, 128 * h + 128, p1=24), v("EC", 0, 128, 16, p1=24))
-        tc(v("c0i"), ps(0, 16, k=b))
-        ts(v("c0j"), v("c0i"), 2047, A.bitwise_and)
-        tt(v("lq"), v("c0j"), v("dlT"), A.subtract)
-        lowest("l", v("lq"), v("nh"))
+            ts(v("has", h, 16, 2), v("SC", 136 * h + 16, 136 * h + 136, 17), 262144.0, A.is_ge)
+            tt(v("lq", h, 16, 2), v("gj", 8 * h, 8 * h + 8), v("dlT", h, 16, 2), A.subtract)
+        ts(v("nh"), v("has"), -1.0, A.mult, 1.0, A.add)
+        bias[0] = BI[0]
+        lowest("l", "GL", v("lq"), v("nh"))
+        bias[0] = BI[1]
         if not last:
-            b = nb(1)
+            b = nb(2)
             mm(ps(0, 256, k=b), v("EA", p1=24), v("XA", p1=24))
-            b2 = nb(1)
-            act(ps(0, 256, k=b2), v("xtl", 0, L), F.Identity, 32768.0)
+            b2 = nb(2)
+            ts(ps(0, 256, k=b2), v("xtl", 0, L), 32768.0, A.add)
             tt(v("YT"), v("TR%d" % t), ps(0, 256, k=b), A.max)
             tt(v("CT"), v("YT"), ps(0, 256, k=b2), A.min)
             ts(v("CTm"), v("CT"), 4095, A.bitwise_and)
@@ -463,6 +467,7 @@ def rank_program(g, core, T, topo):
             scatter(v("xlm"), wl, v("mp", d, d + 64))
             if not last:
                 scatter(v("xtl"), wl, v("CTm", d, d + 64))
+        bias[0] = 0.0
         for h in range(2):
             for q in range(4 * h, 4 * h + 4):
                 a = q % 4
@@ -494,6 +499,7 @@ def rank_program(g, core, T, topo):
             mm(ps(0, 128, k=b), v("I"), v("key"), True, False)
             mm(ps(0, 128, k=b), v("Ih"), halves("hf", h), False, True)
             act(halves("Kh", h), ps(0, 128, k=b))
+        bias[0] = BI[3]
         for h in range(2):
             for q in range(4 * h, 4 * h + 4):
                 ne, p, sx = halves("NE", q, 512), halves("P", q, 512), halves("SX", q, 512)
@@ -510,36 +516,35 @@ def rank_program(g, core, T, topo):
                 mm(ps(i, 128, 16, k=b), v("NE", 2048 * h + i, 2048 * h + 2048, 16), v("PB8"))
             tt(halves("k2", h), ps(0, 128, k=b), halves("Kh", h), A.min)
             scan(halves("SC2", h), v("r16"), halves("k2", h))
-            K8 = [v(z, 8 * h, 8 * h + 8) for z in ("ki", "kj", "IV", "CHL")]
-            tc(K8[0], v("SC2", 128 * h + 15, 128 * h + 128, 16))
-            ts(K8[1], K8[0], 11, A.arith_shift_right, 31, A.bitwise_and)
-            ts(K8[2], K8[1], 1.0, A.max, -1.0, A.mult)
-            b = nb(1)
-            mm(ps(0, 128, p1=8, k=b), K8[2], v("Ih"))
-            act(v("XI", 128 * h, 128 * h + 128, p1=8), ps(0, 128, p1=8, k=b))
-            b = nb(1)
-            mm(ps(0, 8, k=b), v("I"), v("cC"), True, False)
-            todisk(b, 0, "XI", 128 * h, 8, False, "Sel")
-            tc(K8[3], ps(0, 8, k=b))
-            gather("S", halves("CH", h), halves("P", h, 2048), K8[3])
-        ts(v("has"), k15, 0.0, A.is_gt)
-        tt(v("kh"), v("SC2", 15, 256, 16), v("has"), A.mult)
+            tt(v("kh", h, 16, 2), v("SC2", 128 * h + 15, 128 * h + 128, 16), v("has", h, 16, 2), A.mult)
+        bias[0] = 0.0
+        tc(v("ki"), v("SC2", 15, 256, 16))
+        ts(v("kj"), v("ki"), 11, A.arith_shift_right, 31, A.bitwise_and)
+        ts(v("IV"), v("kj"), 1.0, A.max, -1.0, A.mult)
+        b = nb(1)
+        for h in range(2):
+            mm(ps(128 * h, 128 * h + 128, p1=8, k=b), v("IV", 8 * h, 8 * h + 8), v("Ih"))
+        act(v("XI", p1=8), ps(0, 256, p1=8, k=b))
+        b = nb(1)
+        mm(ps(0, 16, k=b), v("I"), v("cC"), True, False)
+        todisk(b, 0, "XI", 0, 16, False, "Sel")
+        tc(v("CHL"), ps(0, 16, k=b))
+        for h in range(2):
+            gather("S", halves("CH", h), halves("P", h, 2048), v("CHL", 8 * h, 8 * h + 8))
         ts(v("dd"), v("kh"), 65536 + 3, A.bitwise_and)
         for d in range(N + 1):
             ts(v("OH", 16 * d, 16 * d + 16), v("dd"), float(65536 + d - 1 if d else 0), A.is_equal)
         b = nb(1)
         mm(ps(0, 80, k=b), v("I"), v("base"), True, False)
-        for d in range(N + 1):
-            mm(ps(16 * d + 8, 16 * d + 16, k=b), o128, v("OH", 16 * d, 16 * d + 8), False, False)
+        mm(ps(1, 80, 2, k=b), o128, v("OH", 0, 80, 2), False, False)
         mm(ps(0, 80, k=b), TRI, v("OH"), False, True)
         tt(v("w3"), ps(0, 80, k=b), v("OH"), A.mult)
         b = nb(1)
         for h in range(2):
-            for d in range(N + 1):
-                mm(ps(128 * h, 128 * h + 128, p1=8, k=b), v("w3", 16 * d + 8 * h, 16 * d + 8 * h + 8), v("Ih"), d == 0, d == N)
-        tc(v("XS", p1=8), ps(0, 256, p1=8, k=b))
+            mm(ps(128 * h, 128 * h + 128, p1=40, k=b), v("w3", h, 80, 2), v("Ih"))
+        tc(v("XS", p1=40), ps(0, 256, p1=40, k=b))
         b = nb(1)
-        todisk(b, 0, "XS", 0, 16, True)
+        todisk(b, 0, "XS", 0, 16, True, rows=40)
         tc(v("SLL"), ps(0, 16, k=b))
         wt = "win%d" % t
         scatter(v(wt), v("SLL"), v("CH"))
@@ -549,7 +554,7 @@ def rank_program(g, core, T, topo):
         got("arr%d" % t, narr, [v(Ln, s * CAP, s * CAP + CAP) for s in others], snd, 3.0)
         if t < RO - 2:
             TR = "TR%d" % (t + 1)
-            b = nb(1)
+            b = nb(2)
             mm(ps(0, 256, k=b), v("R8", p1=8), v("XI", p1=8))
             ts(v("mk"), ps(0, 256, k=b), v("pc", 2, 3), A.not_equal)
             wv = v("wint%d" % t)
@@ -562,7 +567,10 @@ def rank_program(g, core, T, topo):
             ts(v("ch"), v("kh"), 2047, A.bitwise_and)
             ts(v("nn"), v("kh"), 0.0, A.is_gt)
             tt(v("sq"), v("ch"), v("dlT"), A.subtract)
-            lowest("s", v("sq"), v("nn"))
+            bias[0] = BI[2]
+            tc(v("V2s"), v("ch"))
+            tolist("V2s", "XWs", "WAs", 0.0)
+            lowest("s", "WAs", v("sq"), v("nn"))
             for blk in range(3, -1, -1):
                 scatter(v("xsn"), v("WLs", 4 * blk, 4 * blk + 4), v("CH", 64 * blk, 64 * blk + 64))
     ts(v("yfo"), v("L4"), -1.0, A.mult, 255.0, A.add)
@@ -604,7 +612,7 @@ def _emit(g, T, ops):
                     need[j] = max(need.get(j, 0), 1)
                 if hit:
                     k = 2
-                    if same and o["q"] == "T":
+                    if same and (o["q"] == "T" or bf == "order"):
                         k = 1
                     need[j] = max(need.get(j, 0), k)
         for (bf, p0, p1, m, wr) in mine:
@@ -642,7 +650,7 @@ def _emit(g, T, ops):
             if best is None or s < best[0]:
                 best = (s, q)
         s, q = best
-        i = max([z for z in ready[q] if est[z] <= s + 1e-9], key=lambda z: (tail[z], -z))
+        i = max([z for z in ready[q] if est[z] <= s + 1e-9], key=lambda z: (tail[z] + ops[z]["bias"], -z))
         ready[q].remove(i)
         o = ops[i]
         if q != "R":

from concourse.bass import DstId, RemoteDMATransfer
from concourse.mybir import dt, AluOpType as A, AxisListType, ActivationFunctionType as F

N, W, H, L, CAP, RO, SL = 4, 2048, 2048, 256, 56, 4, 224
DUMP = 256
SW = DUMP + N * 256
_B, _F, _H, _I, _U = "bfloat16", "float32", "float16", "int32", "uint16"
_SB = {
    "xlm": (W + L, _B), "xtl": (W + L, _I), "xmo": (4096, _B), "xsn": (H + L, _B), "sn0": (H, _B), "fm0": (L, _B),
    "fr0": (RO * L, _B), "wk0": (3, _I), "wkf": (3, _F), "frs": (N * SL, _B), "win0": (SW, _B), "win1": (SW, _B), "win2": (SW, _B), "win3": (SW, _B),
    "wint0": (SW, _F), "wint1": (SW, _F),
    "L0": (L, _B), "L1": (L, _B), "L2": (L, _B), "L3": (L, _B), "L4": (L, _B), "TR0": (L, _F), "TR1": (L, _F), "TR2": (L, _F), "yfo": (L, _B),
    "mp": (L, _B), "mT": (L, _B), "qT": (L, _B), "au": (32, _I), "am": (32, _I), "up": (16, _I), "av": (48, _I), "ci": (L, _I),
    "cj": (L, _I), "XV": (48, _H), "XA": (256, _H), "ti": (12, _F), "tj": (12, _F), "tk": (12, _F), "tbl": (2304, _B),
    "CL": (L, _U), "X": (4096, _B), "E": (4096, _B), "Y": (4096, _B), "P": (4096, _B), "NE": (4096, _B), "SX": (4096, _B),
    "SC": (272, _F), "gi": (16, _I), "gj": (16, _I), "GV": (16, _H), "XG": (256, _H), "GL": (16, _U), "TG": (L, _U), "xg": (L, _B),
    "hi": (512, _I), "hp": (256, _I), "hq": (256, _I), "hs": (256, _I), "hh": (256, _I), "hf": (256, _H), "HL": (256, _U), "Kh": (256, _F),
    "k2": (256, _F), "SC2": (256, _F), "ki": (16, _I), "kj": (16, _I), "IV": (16, _H), "XI": (256, _B), "CHL": (16, _U), "CH": (L, _B),
    "has": (16, _F), "kh": (16, _I), "ch": (16, _I), "cd": (16, _I), "nc": (16, _I), "dd": (16, _I), "OH": (80, _B),
    "w3": (80, _H), "rin": (N * SL, _B), "XS": (256, _H), "sf": (16, _F), "SLL": (16, _U),
    "TGp": (L, _F), "mk": (L, _F), "YT": (L, _F), "CT": (L, _I), "CTm": (L, _I),
    "nh": (16, _B), "nn": (16, _B), "lq": (16, _F), "sq": (16, _F),
}
for _z in "ls":
    for _k, _v in {"y": (16, _F), "V2": (16, _H), "XW": (256, _H), "WA": (16, _U), "FT0": (L, _B), "FT1": (L, _B), "SCW": (1024, _B), "SCM": (1024, _B), "nd": (16, _F),
                   "z": (16, _F), "V3": (16, _H), "XV": (256, _H), "WL": (16, _U)}.items():
        _SB[_k + _z] = _v
_CO = {
    "one": (512, _B), "I": (128, _B), "nI": (128, _B), "Ih": (128, _H), "bo": (128, _B), "b8": (8, _B), "tmp": (128, _B), "tri": (128, _B),
    "Rep": (512, _B), "RepN": (512, _B), "Sel": (144, _B), "Selh": (144, _H), "i4": (128, _B), "R8": (128, _B), "TR": (128, _B), "key": (128, _B),
    "key18": (136, _B), "r16": (128, _F), "cC": (16, _B), "lane": (16, _F), "base": (80, _B),
    "i5": (40, _B), "mkc": (256, _B), "EC17": (136, _H), "key17": (136, _B), "r17": (136, _F), "pc": (8, _F), "pi": (4, _I), "Wb": (128, _B), "Wt": (16, _B), "cT": (256, _F), "NB8": (8, _B), "PB8": (8, _B),
    "c32": (32, _F), "duT": (16, _F), "dlT": (16, _F), "e0": (128, _F), "e1": (128, _F), "e2": (128, _F), "ek": (128, _F), "ea": (128, _F),
    "EC": (128, _H), "EA": (128, _H),
}
_PACK, _POS = {}, {}
for _k in list(_SB) + list(_CO):
    _n, _t = (_SB.get(_k) or _CO.get(_k))
    if _n <= 64:
        _nn = max(32, (_n + 31) // 32 * 32)
        _o = _PACK.get(_t, 0)
        _POS[_k] = ("pk_" + _t, _o)
        _PACK[_t] = _o + _nn
    else:
        _POS[_k] = ("t_" + _k, 0)
SCRATCH = {}
for _k in list(_SB) + list(_CO):
    _n, _t = (_SB.get(_k) or _CO.get(_k))
    if _n > 64:
        SCRATCH["t_" + _k] = ("sbuf", [128, _n], _t)
for _t, _n in _PACK.items():
    SCRATCH["pk_" + _t] = ("sbuf", [128, _n], _t)
for _k in range(8):
    SCRATCH["ps%d" % _k] = ("psum", [128, 512], "float32")
    _POS["ps%d" % _k] = ("ps%d" % _k, 0)
_QUE = ("V", "S", "T", "G")
SEMAPHORES = ["q" + e for e in _QUE] + ["ld%d" % i for i in range(12)] + ["rarr", "rloc", "st0", "st1"] + \
    ["%s%d" % (p, t) for p in ("arr", "tarr", "loc", "tloc") for t in range(RO)]

GB, EB = "VSSSVVSS", "VVVVSSVS"
GD, ED = "SVSSVSSV", "VSSVSSSV"
SE = "SSVSSVVV"
BI = (-11.0, -8.0, -2.0, -1.0)


def rank_program(g, core, T, topo):
    me = T.rank_of(core)
    if me is None:
        return
    others = [(me + 1 + k) % N for k in range(N - 1)]
    ops = []
    bias = [0.0]

    def v(name, a=None, b=None, step=1, p0=0, p1=128):
        buf, o = _POS[name]
        n = (_SB.get(name) or _CO.get(name) or (512, _F))[0]
        a = 0 if a is None else a
        b = n if b is None else b
        return (buf, p0, p1, o + a, o + b, step)

    def ap(x):
        if x[5] == 1:
            return T[x[0]][x[1]:x[2], x[3]:x[4]]
        return T[x[0]][x[1]:x[2], x[3]:x[4]:x[5]]

    def ncol(x):
        return len(range(x[3], x[4], x[5]))

    def arg(s):
        return ap(s) if isinstance(s, tuple) else s

    def op(q, fn, rd, wr, cost, sem=None, val=0, lag=0.06, after=None, n=1):
        ops.append({"q": q, "fn": fn, "rd": rd, "wr": wr, "cost": cost, "sem": sem, "val": val, "lag": lag, "after": after, "bias": bias[0]})
        return len(ops) - 1

    cyc = 0.00083 * 1.2

    def vc(n, f=1.0):
        return 0.03 + cyc * max(64, n * f)

    two = ("pk_bfloat16", "pk_float16", "pk_uint16")

    def is2(x):
        return x[0] in two or SCRATCH[x[0]][2] in (_B, _H, _U)

    def tc(out, x):
        f = 0.5 if is2(out) and is2(x) else 1.0
        return op("V", lambda: g.vector.tensor_copy(ap(out), ap(x)), [x], [out], vc(ncol(x), f))

    def tt(out, x, y, o):
        f = 1.0 if x[0][:2] == "ps" or y[0][:2] == "ps" else 2.0
        return op("V", lambda: g.vector.tensor_tensor(ap(out), ap(x), ap(y), o), [x, y], [out], vc(ncol(x), f))

    def ts(out, x, s1, o1, s2=None, o2=None):
        f = 0.5 if is2(out) and is2(x) else 1.0
        rd = [x] + [s for s in (s1, s2) if isinstance(s, tuple)]
        if o2 is None:
            return op("V", lambda: g.vector.tensor_scalar(ap(out), ap(x), arg(s1), None, o1), rd, [out], vc(ncol(x), f))
        return op("V", lambda: g.vector.tensor_scalar(ap(out), ap(x), arg(s1), arg(s2), o1, o2), rd, [out], vc(ncol(x), f))

    def scan(out, d0, d1):
        return op("V", lambda: g.vector.tensor_tensor_scan(ap(out), ap(d0), ap(d1), 0.0, A.mult, A.max), [d0, d1], [out], vc(ncol(d1)))

    def vset(out, c):
        return op("V", lambda: g.vector.memset(ap(out), c), [], [out], vc(ncol(out), 0.5))

    def act(out, x, fn=F.Copy, bias=0.0, scale=1.0):
        return op("S", lambda: g.scalar.activation(ap(out), ap(x), fn, bias=arg(bias), scale=arg(scale)),
                  [x] + [s for s in (bias, scale) if isinstance(s, tuple)], [out], 0.06 + cyc * ncol(x))

    def copy(q, out, x):
        return tc(out, x) if q == "V" else act(out, x)

    def gather(q, out, win, off):
        c = 0.06 + cyc * 1.5 * ncol(out)
        if q == "V":
            return op("V", lambda: g.vector.tensor_copy(ap(out), ap(win).indirect(ap(off))), [win, off], [out], c)
        return op("S", lambda: g.scalar.activation(ap(out), ap(win).indirect(ap(off)), F.Copy), [win, off], [out], c)

    def gatherop(out, win, off, y, o):
        return op("V", lambda: g.vector.tensor_tensor(ap(out), ap(win).indirect(ap(off)), ap(y), o), [win, off, y], [out],
                  0.06 + cyc * 1.5 * ncol(out))

    def scatter(win, off, x):
        return op("V", lambda: g.vector.tensor_copy(ap(win).indirect(ap(off)), ap(x)), [x, off], [win], 0.06 + cyc * 3 * ncol(x))

    def mm(out, lhsT, rhs, start=True, stop=True):
        m = ncol(lhsT)
        return op("T", lambda: g.tensor.matmul(ap(out), ap(lhsT), ap(rhs), start, stop), [lhsT, rhs], [out],
                  0.0005 * max(min(64, m), ncol(rhs)))

    def pick(out, x, pattern, cmp, fill, base, cm):
        n = ncol(out)
        return op("G", lambda: g.affine_select(ap(out), ap(x), pattern, cmp, fill, base, cm), [x], [out, pool], 0.2 + cyc * 2 * n)

    def iota(out, pattern, base, cm, small=True):
        def fn():
            if small:
                return g.iota(ap(out), pattern, base, cm, allow_small_or_imprecise_dtypes=True)
            return g.iota(ap(out), pattern, base, cm)
        return op("G", fn, [], [out, pool], 0.15 + cyc * 2 * ncol(out))
    pool = ("pool", 0, 128, 0, 1, 1)

    nld = [0]

    def load(q, out, src, cost):
        s = "ld%d" % nld[0]
        nld[0] += 1
        eng = g.sync if q == "D" else g.scalar
        return op(q, lambda: eng.dma_start(ap(out), src), [], [out, ("order", 0, 128, 0, 1, 2)], 0.08, sem=s, val=16, lag=2.0 + cost)

    bank = [0]

    def ps(a=0, b=512, step=1, p0=0, p1=128, k=None):
        k = bank[0] if k is None else k
        return ("ps%d" % k, p0, p1, a, b, step)

    def nb(kind=0):
        cnt[kind] += 1
        return (cnt[kind] % 2, 2 + cnt[kind] % 4, 6 + cnt[kind] % 2)[kind]
    cnt = {0: 0, 1: 0, 2: 0}

    def fused(name, src, dst, sem, loc, t_lag, after=None):
        eng = topo.engines(core, T.cores[others[0]])
        for d in others:
            eng = [e for e in eng if e in topo.engines(core, T.cores[d])]
        parts, total = [eng[0:len(eng) // 4], eng[len(eng) // 4:len(eng) // 2], eng[len(eng) // 2:]], len(eng)

        def fn():
            tr = []
            for d, es in zip(others, parts):
                rid, pid, _ = topo.addr(T.cores[d])
                m = 0
                for e in es:
                    m |= 1 << e
                tr.append(RemoteDMATransfer(dst_ids=[DstId(rid=rid, pnc=pid)], dma_engine_mask=m, remote_sem=T.sem[sem],
                                            srcs=[ap(src(d))], dsts=[ap(dst(d))], alu_op=0))
            return g.remote_dma_fused(tr, local_sem=T.sem[loc])
        return op("G", fn, [src(d) for d in others], [], 1.0, sem=loc, val=total, lag=1.5)

    def got(sem, total, wr, after, lag):
        return op("R", None, [], wr, 0.0, sem=sem, val=total, lag=lag, after=after)

    def arrivals():
        n = 0
        for s in others:
            od = [(s + 1 + k) % N for k in range(N - 1)]
            eng = topo.engines(T.cores[s], T.cores[od[0]])
            for d in od:
                eng = [e for e in eng if e in topo.engines(T.cores[s], T.cores[d])]
            parts = [eng[0:len(eng) // 4], eng[len(eng) // 4:len(eng) // 2], eng[len(eng) // 2:]]
            n += len(parts[od.index(me)])
        return n
    narr = arrivals()

    def slot(d, name, t):
        return v("%s%d" % (name, t), DUMP + 256 * d, DUMP + 256 * d + CAP)

    load("D", v("fm0"), T.fm[:], 0.5)
    load("D", v("wk0"), T.wk[:], 0.2)
    load("D", v("xlm", 0, W), T.lm[:], 2.0)
    load("D", v("xtl", 0, W), T.tl[:], 5.0)
    load("D", v("xmo"), T.mo[:], 8.0)
    load("D", v("fr0"), T.fr[:], 9.0)
    load("D", v("sn0"), T.sn[:], 11.0)
    vset(v("one", 0, 128), 1.0)
    vset(v("one", 128, 512), 1.0)
    o128 = v("one", 0, 128)
    pick(v("I"), o128, [[-1, 128]], A.is_equal, 0.0, 0, 1)
    pick(v("tmp"), o128, [[-16, 8], [0, 16]], A.is_ge, 0.0, 0, 1)
    pick(v("bo"), v("tmp"), [[16, 8], [0, 16]], A.is_ge, 0.0, 15, -1)
    for k in range(3):
        pick(v("e%d" % k, p1=24), v("one", 0, 128, p1=24), [[-1, 8], [0, 16]], A.is_equal, 0.0, -8 * k, 1)
    pick(v("RepN", p1=32), v("one", 0, 512, p1=32), [[-1, 32], [0, 16]], A.is_equal, 0.0, 0, 1)
    for a in range(4):
        act(v("i4", 32 * a, 32 * a + 32, p1=32), v("I", 0, 32, p1=32))
    b = nb(0)
    mm(ps(k=b), v("i4", p1=32), v("RepN", p1=32))
    act(v("Rep"), ps(k=b))
    act(v("RepN"), ps(k=b), scale=-1.0)
    ts(v("nI"), v("I"), -1.0, A.mult)
    tc(v("Ih"), v("I"))
    tc(v("b8"), v("bo", 0, 128, 16))
    ts(v("NB8"), v("b8"), -8388608.0, A.mult)
    ts(v("PB8"), v("b8"), 131072.0, A.mult)
    iota(v("key"), [[0, 8], [-2048, 16]], 65536 + 32768, 0)
    iota(v("pi", 0, 1), [[0, 1]], 0, 1, False)
    ts(v("pi", 1, 2), v("pi", 0, 1), 15, A.bitwise_and)
    tc(v("pc", 0, 1), v("pi", 1, 2))
    ts(v("pc", 1, 2), v("pc", 0, 1), 0.0, A.is_gt)
    ts(v("pc", 2, 3), v("pc", 0, 1), -16.0, A.add)
    ts(v("pc", 4, 5), v("pc", 1, 2), 65536.0, A.mult)
    ts(v("pi", 3, 4), v("pi", 0, 1), 4, A.arith_shift_right, 1, A.bitwise_and)
    tc(v("pc", 6, 7), v("pi", 3, 4))
    ts(v("pc", 5, 6), v("pc", 6, 7), -1.0, A.mult, 1.0, A.add)
    tc(v("wkf"), v("wk0"))
    ts(v("Wb"), v("bo"), v("wkf", 0, 1), A.mult)
    ts(v("tri"), v("bo"), v("wkf", 1, 2), A.mult)
    ts(v("tmp"), v("I"), v("wkf", 2, 3), A.mult)
    b = nb(1)
    mm(ps(0, 128, p1=24, k=b), v("one", 0, 24), v("tmp"))
    tt(v("ek", p1=24), v("e1", p1=24), ps(0, 128, p1=24, k=b), A.mult)
    tt(v("EC", p1=24), v("ek", p1=24), v("e0", p1=24), A.add)
    ts(v("ea", p1=24), v("e2", p1=24), 2048.0, A.mult)
    tt(v("EA", p1=24), v("ea", p1=24), v("e0", p1=24), A.add)
    vset(v("r16"), 1.0)
    vset(v("r16", 0, 128, 16), 0.0)
    for x in range(2):
        w = v("wkf", x, x + 1)
        ts(v("Wt", 8 * x, 8 * x + 8), v("b8"), w, A.mult, -1.0, A.mult)
        b = nb(1)
        mm(ps(0, 128, k=b), o128, v("Wb") if x == 0 else v("tri"))
        ts(v("cT", 128 * x, 128 * x + 128), ps(0, 128, k=b), 255.0, A.mult)
    b = nb(1)
    mm(ps(0, 16, k=b), o128, v("Wt"))
    for h in range(2):
        ts(v("c32", h, 32, 2), ps(0, 16, k=b), -255.0, A.mult)
    for gr in range(8):
        tc(v("EC17", 17 * gr, 17 * gr + 16, p1=24), v("EC", 16 * gr, 16 * gr + 16, p1=24))
    tc(v("EC17", 16, 136, 17, p1=24), v("EC", 0, 128, 16, p1=24))
    iota(v("key17"), [[0, 8], [-2048, 17]], 32768, 0)
    ts(v("key18"), v("key17"), 128.0, A.mult)
    vset(v("r17"), 1.0)
    vset(v("r17", 0, 136, 17), 0.0)
    pick(v("Sel", p1=8), v("one", 0, 144, p1=8), [[1, 144]], A.is_equal, 0.0, -16, -16)
    for k in range(5):
        act(v("i5", 8 * k, 8 * k + 8, p1=8), v("I", 0, 8, p1=8))
    b = nb(1)
    mm(ps(0, 144, p1=40, k=b), v("i5", p1=8), v("Sel", p1=8))
    tc(v("Selh", p1=40), ps(0, 144, p1=40, k=b))
    iota(v("duT"), [[0, 8], [128, 2]], 1024, 1)
    ts(v("dlT"), v("duT"), 1024.0, A.add)
    iota(v("ti"), [[1, 12]], 0, 0)
    ts(v("tj"), v("ti"), v("pc", 0, 1), A.is_equal)
    ts(v("tk"), v("tj"), 2.0, A.mult, -1.0, A.add)
    vset(v("tbl", 0, 1), -1.0)
    for k in range(12):
        n = min(1 << k, 2304 - (1 << k))
        ts(v("tbl", 1 << k, (1 << k) + n), v("tbl", 0, n), v("tk", k, k + 1), A.max)
    iota(v("lane", 0, 16), [[16, 16]], 0, 0)
    ts(v("lane", 0, 16), v("lane", 0, 16), v("pc", 0, 1), A.add)
    for h in range(2):
        ts(v("cC", 8 * h, 8 * h + 8), v("lane", 0, 8), 16.0, A.mult, 16.0, A.add)
    iota(v("base"), [[256, 5], [0, 16]], 0, 0)
    pick(v("R8", p1=8), v("one", 0, 128, p1=8), [[-1, 8], [0, 16]], A.is_equal, 0.0, 0, 1)
    for t in range(RO - 1):
        o = v("TR%d" % t, SL if t else 0, L)
        act(o, v("one", 0, ncol(o)), F.Identity, 0.0, v("pc", 4, 5))
        for d in range(N):
            if t < RO - 2:
                act(slot(d, "wint", t), v("one", 0, CAP), F.Identity, 0.0, v("pc", 4, 5))
    pick(v("TR"), o128, [[1, 128]], A.is_gt, 0.0, 0, -1)
    ts(v("mkc"), v("one", 0, 256), -7.5, A.mult)
    for a in range(2):
        x = v("mkc", p0=64 * a, p1=64 * a + 64)
        pick(x, x, [[0, 4], [1, 64]], A.is_gt, -100.0, 0, -1)
    TRI = v("TR")
    ts(v("xsn", 0, H), v("sn0"), -1.0, A.mult, 255.0, A.add)

    for s in others + [me]:
        for t in range(RO):
            o = v("frs", s * SL + t * CAP, s * SL + t * CAP + CAP)
            if s == me:
                o = slot(me, "win", t)
            act(o, v("fr0", t * L + s * CAP, t * L + s * CAP + CAP), F.Identity, 255.0, -1.0)
    for t in range(RO):
        act(v("L%d" % (t + 1), SL, L), v("fr0", t * L + SL, t * L + L), F.Identity, 255.0, -1.0)
    snd = fused("r", lambda d: v("frs", d * SL, d * SL + SL), lambda d: v("rin", me * SL, me * SL + SL), "rarr", "rloc", 0)
    got("rarr", narr, [v("rin", s * SL, s * SL + SL) for s in others], snd, 8.0)
    for t in range(RO):
        for s in others:
            act(slot(s, "win", t), v("rin", s * SL + t * CAP, s * SL + t * CAP + CAP))

    ts(v("L0"), v("fm0"), -1.0, A.mult, 255.0, A.add)

    def halves(name, h, n=128):
        return v(name, h * n, h * n + n)

    def todisk(b, c, X, x0, n, first, sel="Selh", rows=8):
        for ll in range(16):
            mm(ps(c, c + n, k=b), v(sel, 16 - ll, 144 - ll, p1=rows), v(X, x0 + ll, x0 + 16 * n, 16, p1=rows), first and ll == 0, ll == 15)

    def tolist(src, xs, out, shift):
        b = nb(2)
        for h in range(2):
            mm(ps(128 * h, 128 * h + 128, p1=8, k=b), ps8(src, h), v("Ih"))
        tc(v(xs, p1=8), ps(0, 256, p1=8, k=b))
        b = nb(2)
        todisk(b, 0, xs, 0, 16, True)
        ts(v(out), ps(0, 16, k=b), shift, A.add)

    def ps8(src, h):
        return v(src, h, 16, 2)

    def lowest(z, places, q, valid):
        for k in range(2):
            x = v("FT%d%s" % (k, z))
            op("S", lambda x=x, k=k: g.scalar.activation(ap(x), ap(v("tbl")).indirect(ap(v(places))), F.Copy, scale=ap(v("pc", 5 + k, 6 + k))),
               [v("tbl"), v(places), v("pc", 5 + k, 6 + k)], [x], 0.06 + cyc * 1.5 * 256)
        tt(v("y" + z), q, valid, A.mult)
        for pair in range(4):
            b, p = nb(2), 32 * pair
            mm(ps(0, 256, k=b), v("I"), v("mkc"), True, False)
            for odd in range(2):
                for lc in range(2):
                    for blk in range(2):
                        c, o = lc * 128 + blk * 64, (odd * 2 + lc) * 64
                        x = v("FT%d%s" % (odd, z), c, c + 64, p0=p, p1=p + 32)
                        mm(ps(o, o + 64, p0=64 * blk, p1=64 * blk + 64, k=b), x, x, False, False)
            mm(ps(0, 256, k=b), v("I"), v("mkc"), False, True)
            act(v("SCW" + z, 256 * pair, 256 * pair + 256), ps(0, 256, k=b), F.Relu)
        b = nb(2)
        for k in range(16):
            for blk in range(2):
                p = 64 * blk
                mm(ps(k, k + 1, p0=p, p1=p + 64, k=b), v("SCW" + z, 64 * k, 64 * k + 64, p0=p, p1=p + 64),
                   (valid[0], p, p + 64, valid[3] + k, valid[3] + k + 1, 1))
        ts(v("nd" + z), ps(0, 16, k=b), 0.5, A.is_lt)
        tt(v("z" + z), v("y" + z), v("nd" + z), A.mult)
        tt(v("V3" + z), v("z" + z), v("duT"), A.add)
        tolist("V3" + z, "XV" + z, "WL" + z, 1024.0)

    for t in range(RO):
        last = t == RO - 1
        Lt, Ln = "L%d" % t, "L%d" % (t + 1)
        bias[0] = 0.0
        b = nb(1)
        for h in range(2):
            mm(ps(h, 32, 2, k=b), halves(Lt, h), v("Wt"))
        tt(v("au"), ps(0, 32, k=b), v("c32"), A.add)
        ts(v("am"), v("au"), 4095, A.bitwise_and)
        tt(v("up"), v("am", 0, 16), v("am", 16, 32), A.mult)
        ts(v("av", 0, 16), v("up"), 5, A.arith_shift_right, 2047, A.bitwise_and)
        ts(v("av", 16, 32), v("am", 0, 16), 2047, A.bitwise_and)
        ts(v("av", 32, 48), v("up"), 16, A.arith_shift_right, 1, A.bitwise_and)
        tc(v("XV"), v("av"))
        for h in range(2):
            act(halves("mp", h), halves(Lt, h), F.Identity, 255.0, -1.0)
            b2 = nb(1)
            mm(ps(0, 128, k=b2), halves("mp", h), v("I"))
            act(halves("mT", h), ps(0, 128, k=b2))
            b = nb(1)
            mm(ps(0, 128, p1=24, k=b), v("XV", h, 48, 2), v("Ih"))
            xa = v("XA", 128 * h, 128 * h + 128, p1=24)
            tc(xa, ps(0, 128, p1=24, k=b))
            b = nb(1)
            mm(ps(0, 128, k=b), v("EC", p1=24), xa)
            tc(halves("ci", h), ps(0, 128, k=b))
            ts(halves("cj", h), halves("ci", h), 2047, A.bitwise_and)
            tc(halves("CL", h), halves("cj", h))
        for h in range(2):
            for q in range(4 * h, 4 * h + 4):
                a = q % 4
                x, e, off = halves("X", q, 512), halves("E", q, 512), halves("CL", q, 32)
                gather(GB[q], x, v("xlm", 0, W), off)
                mt = v("mT", h * 128, h * 128 + 128, p0=32 * a, p1=32 * a + 32)
                b = nb(0)
                if EB[q] == "V":
                    mm(ps(k=b), mt, v("Rep", p0=32 * a, p1=32 * a + 32))
                    tt(e, x, ps(k=b), A.is_gt)
                else:
                    mm(ps(k=b), mt, v("RepN", p0=32 * a, p1=32 * a + 32), True, False)
                    mm(ps(k=b), v("I"), x, False, True)
                    act(e, ps(k=b), F.Relu)
            b = nb(1)
            mm(ps(0, 136, k=b), v("I"), v("key18"), True, False)
            for i in range(16):
                mm(ps(i, 136, 17, k=b), v("E", 2048 * h + i, 2048 * h + 2048, 16), v("NB8"), False, False)
            mm(ps(0, 136, k=b), v("XA", 128 * h, 128 * h + 128, p1=24), v("EC17", p1=24), False, True)
            scan(halves("SC", h, 136), v("r17"), ps(0, 136, k=b))
            G8 = [v(z, 8 * h, 8 * h + 8) for z in ("gi", "gj", "GV", "GL")]
            tc(G8[0], v("SC", 136 * h + 16, 136 * h + 136, 17))
            ts(G8[1], G8[0], 2047, A.bitwise_and)
            tc(G8[2], G8[1])
            b = nb(1)
            mm(ps(0, 128, p1=8, k=b), G8[2], v("Ih"))
            tc(v("XG", 128 * h, 128 * h + 128, p1=8), ps(0, 128, p1=8, k=b))
            b = nb(1)
            todisk(b, 0, "XG", 128 * h, 8, True)
            tc(G8[3], ps(0, 8, k=b))
            gather("V", halves("TG", h), v("xtl", 0, W), G8[3])
            gather("S", halves("xg", h), v("xlm", 0, W), G8[3])
            b = nb(1)
            mm(ps(0, 128, k=b), halves("xg", h), v("I"), True, False)
            mm(ps(0, 128, k=b), halves("mp", h), v("nI"), False, True)
            act(halves("qT", h), ps(0, 128, k=b))
        if t < RO - 2:
            ts(v("TGp"), v("TG"), 8192.0, A.add)
        for h in range(2):
            ts(v("has", h, 16, 2), v("SC", 136 * h + 16, 136 * h + 136, 17), 262144.0, A.is_ge)
            tt(v("lq", h, 16, 2), v("gj", 8 * h, 8 * h + 8), v("dlT", h, 16, 2), A.subtract)
        ts(v("nh"), v("has"), -1.0, A.mult, 1.0, A.add)
        bias[0] = BI[0]
        lowest("l", "GL", v("lq"), v("nh"))
        bias[0] = BI[1]
        if not last:
            b = nb(2)
            mm(ps(0, 256, k=b), v("EA", p1=24), v("XA", p1=24))
            b2 = nb(2)
            ts(ps(0, 256, k=b2), v("xtl", 0, L), 32768.0, A.add)
            tt(v("YT"), v("TR%d" % t), ps(0, 256, k=b), A.max)
            tt(v("CT"), v("YT"), ps(0, 256, k=b2), A.min)
            ts(v("CTm"), v("CT"), 4095, A.bitwise_and)
        for blk in range(3, -1, -1):
            d = 64 * blk
            wl = v("WLl", 4 * blk, 4 * blk + 4)
            scatter(v("xlm"), wl, v("mp", d, d + 64))
            if not last:
                scatter(v("xtl"), wl, v("CTm", d, d + 64))
        bias[0] = 0.0
        for h in range(2):
            for q in range(4 * h, 4 * h + 4):
                a = q % 4
                y, p = halves("Y", q, 512), halves("P", q, 512)
                gather(GD[q], y, v("xmo"), halves("TG", q, 32))
                b = nb(0)
                mm(ps(k=b), v("qT", h * 128, h * 128 + 128, p0=32 * a, p1=32 * a + 32), v("Rep", p0=32 * a, p1=32 * a + 32), True, False)
                mm(ps(k=b), v("nI"), y, False, True)
                if ED[q] == "V":
                    ts(p, ps(k=b), 255.0, A.add, 0.0, A.max)
                else:
                    act(p, ps(k=b), F.Relu, 255.0)
            b = nb(1)
            for i in range(16):
                mm(ps(i, 256, 16, k=b), v("P", 2048 * h + i, 2048 * h + 2048, 16), v("Wt"))
            u = halves("hi", h, 256)
            tt(u, ps(0, 256, k=b), v("cT"), A.add)
            ts(u, u, 4095, A.bitwise_and)
            u0, u1 = v("hi", 256 * h, 256 * h + 128), v("hi", 256 * h + 128, 256 * h + 256)
            tt(halves("hp", h), u0, u1, A.mult)
            ts(halves("hq", h), halves("hp", h), 5, A.arith_shift_right)
            tt(halves("hs", h), halves("hq", h), u0, A.add)
            ts(halves("hh", h), halves("hs", h), 2047, A.bitwise_and)
            tc(halves("hf", h), halves("hh", h))
            b = nb(1)
            mm(ps(0, 128, k=b), halves("hf", h), v("Ih"))
            tc(halves("HL", h), ps(0, 128, k=b))
            b = nb(1)
            mm(ps(0, 128, k=b), v("I"), v("key"), True, False)
            mm(ps(0, 128, k=b), v("Ih"), halves("hf", h), False, True)
            act(halves("Kh", h), ps(0, 128, k=b))
        bias[0] = BI[3]
        for h in range(2):
            for q in range(4 * h, 4 * h + 4):
                ne, p, sx = halves("NE", q, 512), halves("P", q, 512), halves("SX", q, 512)
                if SE[q] == "V":
                    gatherop(ne, v("xsn", 0, H), halves("HL", q, 32), p, A.not_equal)
                else:
                    gather("S", sx, v("xsn", 0, H), halves("HL", q, 32))
                    b = nb(0)
                    mm(ps(k=b), v("nI"), p, True, False)
                    mm(ps(k=b), v("I"), sx, False, True)
                    act(ne, ps(k=b), F.Abs)
            b = nb(1)
            for i in range(16):
                mm(ps(i, 128, 16, k=b), v("NE", 2048 * h + i, 2048 * h + 2048, 16), v("PB8"))
            tt(halves("k2", h), ps(0, 128, k=b), halves("Kh", h), A.min)
            scan(halves("SC2", h), v("r16"), halves("k2", h))
            tt(v("kh", h, 16, 2), v("SC2", 128 * h + 15, 128 * h + 128, 16), v("has", h, 16, 2), A.mult)
        bias[0] = 0.0
        tc(v("ki"), v("SC2", 15, 256, 16))
        ts(v("kj"), v("ki"), 11, A.arith_shift_right, 31, A.bitwise_and)
        ts(v("IV"), v("kj"), 1.0, A.max, -1.0, A.mult)
        b = nb(1)
        for h in range(2):
            mm(ps(128 * h, 128 * h + 128, p1=8, k=b), v("IV", 8 * h, 8 * h + 8), v("Ih"))
        act(v("XI", p1=8), ps(0, 256, p1=8, k=b))
        b = nb(1)
        mm(ps(0, 16, k=b), v("I"), v("cC"), True, False)
        todisk(b, 0, "XI", 0, 16, False, "Sel")
        tc(v("CHL"), ps(0, 16, k=b))
        for h in range(2):
            gather("S", halves("CH", h), halves("P", h, 2048), v("CHL", 8 * h, 8 * h + 8))
        ts(v("dd"), v("kh"), 65536 + 3, A.bitwise_and)
        for d in range(N + 1):
            ts(v("OH", 16 * d, 16 * d + 16), v("dd"), float(65536 + d - 1 if d else 0), A.is_equal)
        b = nb(1)
        mm(ps(0, 80, k=b), v("I"), v("base"), True, False)
        mm(ps(1, 80, 2, k=b), o128, v("OH", 0, 80, 2), False, False)
        mm(ps(0, 80, k=b), TRI, v("OH"), False, True)
        tt(v("w3"), ps(0, 80, k=b), v("OH"), A.mult)
        b = nb(1)
        for h in range(2):
            mm(ps(128 * h, 128 * h + 128, p1=40, k=b), v("w3", h, 80, 2), v("Ih"))
        tc(v("XS", p1=40), ps(0, 256, p1=40, k=b))
        b = nb(1)
        todisk(b, 0, "XS", 0, 16, True, rows=40)
        tc(v("SLL"), ps(0, 16, k=b))
        wt = "win%d" % t
        scatter(v(wt), v("SLL"), v("CH"))
        mine = (me * CAP, me * CAP + CAP)
        snd = fused("m", lambda d, t=t: slot(d, "win", t), lambda d, Ln=Ln: v(Ln, mine[0], mine[1]), "arr%d" % t, "loc%d" % t, 0)
        act(v(Ln, mine[0], mine[1]), slot(me, "win", t))
        got("arr%d" % t, narr, [v(Ln, s * CAP, s * CAP + CAP) for s in others], snd, 3.0)
        if t < RO - 2:
            TR = "TR%d" % (t + 1)
            b = nb(2)
            mm(ps(0, 256, k=b), v("R8", p1=8), v("XI", p1=8))
            ts(v("mk"), ps(0, 256, k=b), v("pc", 2, 3), A.not_equal)
            wv = v("wint%d" % t)
            op("V", lambda wv=wv: g.vector.tensor_tensor(ap(wv).indirect(ap(v("SLL"))), ap(v("TGp")), ap(v("mk")), A.mult),
               [v("SLL"), v("TGp"), v("mk")], [wv], 0.06 + cyc * 3 * 256)
            snd = fused("t", lambda d, t=t: slot(d, "wint", t), lambda d, TR=TR: v(TR, mine[0], mine[1]), "tarr%d" % t, "tloc%d" % t, 0)
            act(v(TR, mine[0], mine[1]), slot(me, "wint", t))
            got("tarr%d" % t, narr, [v(TR, s * CAP, s * CAP + CAP) for s in others], snd, 4.0)
        if not last:
            ts(v("ch"), v("kh"), 2047, A.bitwise_and)
            ts(v("nn"), v("kh"), 0.0, A.is_gt)
            tt(v("sq"), v("ch"), v("dlT"), A.subtract)
            bias[0] = BI[2]
            tc(v("V2s"), v("ch"))
            tolist("V2s", "XWs", "WAs", 0.0)
            lowest("s", "WAs", v("sq"), v("nn"))
            for blk in range(3, -1, -1):
                scatter(v("xsn"), v("WLs", 4 * blk, 4 * blk + 4), v("CH", 64 * blk, 64 * blk + 64))
    ts(v("yfo"), v("L4"), -1.0, A.mult, 255.0, A.add)
    op("D", lambda: g.sync.dma_start(T.yf[:], ap(v("yfo"))), [v("yfo")], [], 0.08, sem="st0", val=16, lag=2.0)
    op("D", lambda: g.sync.dma_start(T.yl[:], ap(v("xlm", 0, W))), [v("xlm", 0, W)], [], 0.08, sem="st1", val=16, lag=2.0)
    _emit(g, T, ops)


def _emit(g, T, ops):
    nop = len(ops)
    acc, deps = {}, [None] * nop

    def mask(x):
        if x[5] == 1:
            return ((1 << (x[4] - x[3])) - 1) << x[3]
        m = 0
        for c in range(x[3], x[4], x[5]):
            m |= 1 << c
        return m
    memo = {}
    for i, o in enumerate(ops):
        need = {}
        mine = []
        for wr, lst in ((0, o["rd"]), (1, o["wr"])):
            for x in lst:
                if x not in memo:
                    memo[x] = mask(x)
                mine.append((x[0], x[1], x[2], memo[x], wr))
        for (bf, p0, p1, m, wr) in mine:
            for (j, q0, q1, mj, wj) in acc.get(bf, ()):
                if j == i:
                    continue
                same = ops[j]["q"] == o["q"]
                if bf[:2] == "ps":
                    hit = not same or ((wr or wj) and (m & mj) and p0 < q1 and q0 < p1)
                else:
                    hit = (wr or wj) and (m & mj) and p0 < q1 and q0 < p1
                if not hit and bf[:2] == "ps":
                    need[j] = max(need.get(j, 0), 1)
                if hit:
                    k = 2
                    if same and (o["q"] == "T" or bf == "order"):
                        k = 1
                    need[j] = max(need.get(j, 0), k)
        for (bf, p0, p1, m, wr) in mine:
            old = acc.get(bf, [])
            if bf[:2] == "ps":
                old = [z for z in old if z[0] == i]
            elif wr:
                old = [z for z in old if not (z[0] != i and (z[3] | m) == m and p0 <= z[1] and z[2] <= p1)]
            acc[bf] = old + [(i, p0, p1, m, wr)]
        if o["after"] is not None:
            need[o["after"]] = max(need.get(o["after"], 0), 1)
        deps[i] = need
    tail = [0.0] * nop
    succ = [[] for _ in range(nop)]
    for i in range(nop):
        for j in deps[i]:
            succ[j].append(i)
    for i in range(nop - 1, -1, -1):
        o = ops[i]
        tail[i] = o["cost"] + max([tail[j] + o["lag"] for j in succ[i]] + [0.0])
    left = [len(d) for d in deps]
    est = [0.0] * nop
    ready = {}
    for i in range(nop):
        if left[i] == 0:
            ready.setdefault(ops[i]["q"], []).append(i)
    clock, order, done = {}, [], 0
    while done < nop:
        best = None
        for q, lst in ready.items():
            if not lst:
                continue
            c = clock.get(q, 0.0)
            s = max(c, min(est[i] for i in lst)) if q != "R" else min(est[i] for i in lst)
            if best is None or s < best[0]:
                best = (s, q)
        s, q = best
        i = max([z for z in ready[q] if est[z] <= s + 1e-9], key=lambda z: (tail[z] + ops[z]["bias"], -z))
        ready[q].remove(i)
        o = ops[i]
        if q != "R":
            clock[q] = s + o["cost"]
        order.append(i)
        done += 1
        for j in succ[i]:
            e = s + o["cost"] + (o["lag"] if q != "R" and (deps[j][i] == 2 or q == "G") else 0.0)
            if ops[j]["q"] == "R":
                e = s + o["cost"] + ops[j]["lag"]
            est[j] = max(est[j], e)
            left[j] -= 1
            if left[j] == 0:
                ready.setdefault(ops[j]["q"], []).append(j)
    queue = {"V": g.vector, "S": g.scalar, "T": g.tensor, "G": g, "D": g.sync}
    count = {}
    know = {q: {} for q in queue}
    tok, kn = [None] * nop, [None] * nop
    for i in order:
        o = ops[i]
        q = o["q"]
        if q == "R":
            tok[i] = (o["sem"], o["val"])
            kn[i] = {o["sem"]: o["val"]}
            continue
        k = know[q]
        want = {}
        for j, kind in deps[i].items():
            if kind == 2:
                s, val = tok[j]
                if k.get(s, 0) < val and (s not in want or want[s][0] < val):
                    want[s] = (val, j)
        for s in list(want):
            if any(z != s and kn[want[z][1]].get(s, 0) >= want[s][0] for z in want):
                del want[s]
        for s, (val, j) in want.items():
            queue[q].wait_ge(T.sem[s], val)
        for s, (val, j) in want.items():
            for z, n in kn[j].items():
                if k.get(z, 0) < n:
                    k[z] = n
        ins = o["fn"]()
        if o["sem"] is None:
            s = "q" + q
            count[s] = count.get(s, 0) + 1
            ins.then_inc(T.sem[s], 1)
            tok[i] = (s, count[s])
        else:
            tok[i] = (o["sem"], o["val"])
            if q == "D":
                ins.then_inc(T.sem[o["sem"]], 16)
        kn[i] = dict(k)
        kn[i][tok[i][0]] = tok[i][1]
    k = know["G"]
    fin = {}
    for i in range(nop):
        if tok[i][1] > fin.get(tok[i][0], 0):
            fin[tok[i][0]] = tok[i][1]
    for s, n in fin.items():
        if k.get(s, 0) < n:
            g.wait_ge(T.sem[s], n)
